import numpy as np, ml_dtypes
CORES = [5,29,101,125,133,157,229,253]
N = 8
import mx_ref
BF = ml_dtypes.bfloat16
def gentries(a):
    return np.ascontiguousarray(a.reshape(8, 16, -1).transpose(0, 2, 1)).reshape(8, -1)
def gtable(e):
    e = np.asarray(e); return np.ascontiguousarray(e.reshape(8, -1, 16).transpose(0, 2, 1)).reshape(128, -1).astype(np.int32)
def gcols(t, e):
    v = np.concatenate([t.reshape(8, 16, -1, 4), np.zeros((8, 16, 1, 4), BF)], axis=2)
    return np.ascontiguousarray(np.stack([v[g][:, e[g]] for g in range(8)])).reshape(128, -1)
def tile(rs):
    return np.stack(rs, axis=2).reshape(128, -1).astype(BF)
def cut(t, i, w=512):
    return t[:, w * i:w * i + w]
def pick(q, e):
    c = np.concatenate([q[0].reshape(128, -1, 4), np.zeros((128, 1, 4), np.uint8)], axis=1); s = np.concatenate([q[1], np.ones((16, 1), np.uint8)], axis=1)
    return (np.ascontiguousarray(c[:, e].reshape(128, -1)), np.ascontiguousarray(s[:, e]))
def join(*qs):
    return (np.concatenate([q[0] for q in qs], axis=1), np.concatenate([q[1] for q in qs], axis=1))
def put(q, e, v):
    c, s = q[0].reshape(128, -1, 4).copy(), q[1].copy(); c[:, e] = v[0].reshape(128, -1, 4); s[:, e] = v[1]
    return (c.reshape(128, -1), s)
def pk(c, s):
    return (np.ascontiguousarray(c), mx_ref.live(s))
def emit(q):
    return q[0], q[1]
def packed(v, rng):
    q = [mx_ref.quantize(np.ascontiguousarray(v[r])) for r in range(N)]
    return np.stack([a for a, b in q]), np.stack([mx_ref.plane(b, rng) for a, b in q])
def values_of_codes():
    e, c = np.zeros((128, 128, 4), np.float32), np.zeros((128, 2, 4), np.uint8)
    e[np.arange(128), np.arange(128), 0] = 1
    c[:127, :, 0] = np.arange(256).reshape(2, 128).T[:127]
    return mx_ref.matmul(mx_ref.quantize(e.reshape(128, 512).astype(BF)), (c.reshape(128, 8), np.full((16, 2), 127, np.uint8))).T.reshape(-1).astype(np.float64)
CODE_VALUE, SCALE_VALUE = values_of_codes(), 2.0 ** (np.arange(256) - 127.0)
def decode(q):
    return (CODE_VALUE[q[0]].reshape(16, 8, -1, 4) * SCALE_VALUE[q[1]][:, None, :, None] + 0.0).reshape(128, -1).astype(np.float32)
def f(rng, *shape):
    return mx_ref.flush((rng.standard_normal(shape, dtype=np.float32) * np.exp2(rng.integers(-2, 3, shape[:-1] + (1,)))).astype(BF))
def wide(rng, *shape, cols=0):
    v = rng.standard_normal(shape, dtype=np.float32) * np.exp2(rng.integers(-12, 13, shape)).astype(np.float32)
    if cols: v *= np.repeat(np.exp2(rng.integers(-cols, cols + 1, shape[:-2] + (1, shape[-1] // 4))) * (rng.random(shape[:-2] + (1, shape[-1] // 4)) > 0.0625), 4, axis=-1).astype(np.float32)
    return mx_ref.flush(v.astype(BF))
T, P, H = 384, 448, 3
def trim(v):
    v = v.astype(np.float32)
    v[np.abs(v) < np.float32(2.0 ** -16)] = 0
    return v.astype(BF)
def numbers_of(rng):
    return {"x": trim(f(rng, N, 128, 4 * T)), "k": trim(f(rng, N, 128, 4 * P)), "u": np.array(f(rng, N, 128, 512)), "v": np.array(f(rng, N, 128, 512))}
def weights(rng, w):
    c, p = packed(np.stack([w] * N), rng)
    return {"wc": c, "ws": p}
def still(rng):
    w = np.zeros((128, 4, 128, 4), np.float32)
    i = np.arange(128)
    for b in range(4): w[i, b, i, b] = 32
    return weights(rng, w.reshape(128, 2048).astype(BF))
def chase(nx, e):
    return {"nx": np.ascontiguousarray(nx).astype(np.int32), "st": np.stack([gtable(e[r]) for r in range(N)])}
def setup_inputs(rng):
    return {**numbers_of(rng), **weights(rng, np.array(f(rng, 128, 2048))), **chase(rng.integers(0, P, (N, 8, 2 * P)), rng.integers(0, P, (N, 8, T)))}
def setup_inputs_ties(rng):
    d = numbers_of(rng)
    x, k, u = d["x"].reshape(N, 128, T, 4), d["k"].reshape(N, 128, P, 4), d["u"].reshape(N, 128, 128, 4)
    k[:, :, ::2] = 0
    c = np.stack([rng.permutation(T) % 4 for r in range(N)])
    e = rng.integers(0, P, (N, 8, T))
    e = np.where(c[:, None, :] == 1, e // 2 * 2, e)
    for r in range(N):
        for g in rng.permutation(8)[:2]: u[r, :, 16 * g] = 0
        o = gcols(k[r].reshape(128, 4 * P), e[r]).reshape(128, T, 4)
        o = (np.float32(0.0) - o.astype(np.float32)).astype(BF)
        x[r][:, c[r] == 1] = 0
        x[r][:, c[r] == 2] = o[:, c[r] == 2]
    a = rng.integers(0, P, (N, 8, P))
    a = np.where(np.arange(P) % 2 == 0, a // 2 * 2, a)
    b = (a + 2 * rng.integers(1, P // 2, (N, 8, P))) % P
    return {"x": x.reshape(N, 128, 4 * T), "k": k.reshape(N, 128, 4 * P), "u": u.reshape(N, 128, 512), "v": d["v"], **weights(rng, np.array(f(rng, 128, 2048))), **chase(np.stack([a, b], axis=3).reshape(N, 8, 2 * P), e)}
def setup_inputs_sizes(rng):
    def columns(c):
        tiny = c % 2 == 0
        s = np.where(tiny, 2.0 ** -29, 2.0 ** 30) * np.where(c >= 2, -1.0, 1.0)
        a = 0.55 + 0.4 * rng.random((N, 128, c.shape[1], 4))
        a[:, ::16, :, 0] = np.where(tiny[:, None, :], 0.5625, a[:, ::16, :, 0])
        a[:, 8::16, :, 0] = np.where(tiny[:, None, :], 0.625, a[:, 8::16, :, 0])
        return (a * s[:, None, :, None]).astype(np.float32).astype(BF).reshape(N, 128, 4 * c.shape[1])
    d = numbers_of(rng)
    c = np.stack([rng.permutation(T) % 4 for r in range(N)])
    i = np.arange(P) % 4
    u = d["u"].reshape(N, 128, 128, 4)
    u[:, :, ::16] = 0
    for r in range(N):
        o = rng.permutation(8)
        for g in range(8):
            s = 1.0 if o[g] % 2 == 0 else -1.0
            if o[g] < 4:
                u[r, 16 * g, 16 * g, 0] = s * 1.125 * 2.0 ** -30
                u[r, 16 * g + 8, 16 * g, 0] = -s * 2.0 ** -30
            else: u[r, :, 16 * g] = (s * 2.0 ** 30 * (0.55 + 0.4 * rng.random((128, 4)))).astype(np.float32).astype(BF)
    a = 4 * rng.integers(0, P // 4, (N, 8, P)) + i
    b = (a + 4 * rng.integers(1, P // 4, (N, 8, P))) % P
    e = 4 * rng.integers(0, P // 4, (N, 8, T)) + c[:, None, :]
    return {"x": columns(c), "k": columns(np.stack([i] * N)), "u": u.reshape(N, 128, 512), "v": d["v"], **still(rng), **chase(np.stack([a, b], axis=3).reshape(N, 8, 2 * P), e)}
def setup_inputs_crowd(rng):
    d = setup_inputs(rng)
    o = rng.permutation(8)
    h = rng.permutation(N)
    full = h < N // 2
    nx, e = np.zeros((N, 8, P, 2), int), np.zeros((N, 8, T), int)
    for r in range(N):
        for g in range(8):
            nx[r, g] = rng.permutation(P)[:, None] if o[g] < 4 else rng.integers(0, 2, (P, 2)) * (P - 1)
            e[r, g] = rng.permutation(P)[:T] if full[r] else h[r] % 2 * (P - 1)
    return {**d, **chase(nx.reshape(N, 8, 2 * P), e)}
def setup_inputs_spread(rng):
    d = setup_inputs(rng)
    d["x"] = trim(wide(rng, N, 128, 4 * T, cols=6))
    d["k"] = trim(wide(rng, N, 128, 4 * P, cols=6))
    return d
def check_inputs(d):
    b = []
    for n in ("x", "k", "u", "v"):
        a = np.abs(d[n].astype(np.float32))
        if not (np.isfinite(a).all() and ((a == 0) | (a >= 2.0 ** -30) & (a <= 2.0 ** 30)).all()): b.append("a value of " + n)
    for n in ("nx", "st"):
        if ((d[n] < 0) | (d[n] >= P)).any(): b.append("an entry of " + n)
    if (d["wc"] != d["wc"][:1]).any(): b.append("wc differs between ranks")
    s = [mx_ref.live(p) for p in d["ws"]]
    if any((p != s[0]).any() for p in s): b.append("ws differs between ranks")
    return b
def reference(x, k, u, v, wc, ws, nx, st):
    w = pk(wc[0], ws[0])
    lay = [pick(w, np.arange(128 * b, 128 * b + 128)) for b in range(4)]
    qu = [mx_ref.quantize(u[r]) for r in range(N)]
    nodes = decode(join(*[mx_ref.quantize(k[r]) for r in range(N)])).astype(BF)
    now = [mx_ref.quantize(x[r]) for r in range(N)]
    p = [gentries(st[r]) for r in range(N)]
    for t in range(H):
        was = decode(join(*now))
        for r in range(N):
            m = (r + t) % N
            n = gcols(cut(nodes, m, 4 * P), p[r]).astype(np.float32)
            q = mx_ref.quantize(np.ascontiguousarray(((cut(was, r, 4 * T) + n) * np.float32(0.5)).astype(BF)))
            c = mx_ref.matmul(qu[m], q)[::16]
            p[r] = np.take_along_axis(nx[m], 2 * p[r] + (c > 0), axis=1)
            now[r] = mx_ref.quantize(tile([mx_ref.matmul(lay[b], q) * np.float32(0.03125) for b in range(4)]))
    y, pl = np.zeros((N, 128, T), np.float32), np.zeros((N, 8, T), np.float32)
    oc, osc = np.zeros((N, 128, 4 * T), np.uint8), np.zeros((N, 16, T), np.uint8)
    for r in range(N):
        y[r] = mx_ref.matmul(mx_ref.quantize(v[r]), now[r])
        pl[r] = p[r]
        oc[r], osc[r] = emit(now[r])
    return {"y": y, "pl": pl, "oc": oc, "osc": osc}

@@ -1,0 +1,495 @@
+from concourse.bass import DstId, RemoteDMATransfer
+from concourse.mybir import dt, AluOpType, ActivationFunctionType
+
+N, TOK, P, HOPS = 8, 384, 448, 3
+WORLD = 256
+CH = 192
+NCH = TOK // CH
+NL = CH // 16
+NB = CH // 32
+HALF, QUART = P // 2, P // 4
+SEG = P // 16
+NXW = 2 * P * 8 // 512
+FAR, CUT = 256, 600
+ZW, TW = CH + 32, 2 * CH + 32
+CODE, BF, F32, I32, U16, U8 = "float8_e4m3fn_x4", "bfloat16", "float32", "int32", "uint16", "uint8"
+
+SCRATCH = {
+    "xin": ("sbuf", [128, 4 * TOK], BF), "kin": ("sbuf", [128, 4 * P], BF),
+    "uin": ("sbuf", [128, 512], BF), "vin": ("sbuf", [128, 512], BF),
+    "wq": ("sbuf", [128, 512], CODE), "wp": ("sbuf", [128, 512], U8),
+    "nxi": ("sbuf", [128, 2 * SEG], I32), "sti": ("sbuf", [128, TOK // 16], I32),
+    "kq": ("sbuf", [128, P], CODE), "kp": ("sbuf", [128, P], U8),
+    "uq": ("sbuf", [128, 128], CODE), "up": ("sbuf", [128, 128], U8),
+    "u0q": ("sbuf", [128, 128], CODE), "u0p": ("sbuf", [128, 128], U8),
+    "u1q": ("sbuf", [128, 128], CODE), "u1p": ("sbuf", [128, 128], U8),
+    "u2q": ("sbuf", [128, 128], CODE), "u2p": ("sbuf", [128, 128], U8),
+    "k1q": ("sbuf", [128, P], CODE), "k1p": ("sbuf", [128, P], U8),
+    "k2q": ("sbuf", [128, P], CODE), "k2p": ("sbuf", [128, P], U8),
+    "vq": ("sbuf", [128, 128], CODE), "vp": ("sbuf", [128, 128], U8),
+    "nd0": ("dram", [4, 128, NXW], I32), "nd1": ("dram", [4, 128, NXW], I32), "nd2": ("dram", [4, 128, NXW], I32),
+    "stg": ("sbuf", [128, 2 * P + 4], I32), "nxf": ("sbuf", [128, 2 * SEG], F32),
+    "win0": ("sbuf", [128, P], BF), "win1": ("sbuf", [128, P], BF), "win2": ("sbuf", [128, 2 * P], F32),
+    "dia": ("sbuf", [128, 384], BF), "eye": ("sbuf", [128, 128], BF),
+    "cst": ("sbuf", [128, 96], F32), "cstt": ("sbuf", [128, 96], F32),
+    "rep": ("sbuf", [128, 8], I32), "repo": ("sbuf", [128, 8], U16), "wrap": ("sbuf", [128, 4], U16),
+    "et": ("sbuf", [128, 2048], BF), "eq": ("sbuf", [128, 1536], CODE), "ep": ("sbuf", [128, 1536], U8),
+    "o0": ("sbuf", [128, 5 * TOK // 16], U16), "off": ("sbuf", [128, 48 * NCH], U16),
+    "nt": ("sbuf", [128, 4 * TOK], BF), "vt": ("sbuf", [128, 4 * TOK], BF), "rt": ("sbuf", [128, 4 * TOK], BF),
+    "nq": ("sbuf", [128, TOK], CODE), "npl": ("sbuf", [128, TOK], U8),
+    "bq": ("sbuf", [128, TOK], CODE), "bp": ("sbuf", [128, TOK], U8),
+    "sq": ("sbuf", [128, TOK], CODE), "sp": ("sbuf", [128, TOK], U8),
+    "pq": ("sbuf", [128, 2 * TOK], CODE), "ppl": ("sbuf", [128, 2 * TOK], U8),
+    "sel": ("sbuf", [128, TOK], BF), "zz": ("sbuf", [128, ZW * NCH], BF), "tt": ("sbuf", [128, TW * NCH], BF),
+    "pw": ("sbuf", [128, 32 * NCH], F32), "bd": ("sbuf", [128, TOK], F32), "plb": ("sbuf", [128, TOK], F32),
+    "yb": ("sbuf", [128, TOK], F32),
+    "hq": ("sbuf", [128, HALF], CODE), "hp": ("sbuf", [128, P], U8),
+    "huq": ("sbuf", [128, 128], CODE), "hup": ("sbuf", [128, 128], U8), "hnx": ("dram", [2, 128, NXW], I32),
+    "ps": ("psum", [128, 4096], F32),
+}
+
+ALU, ACT = AluOpType, ActivationFunctionType
+
+PLAN = """
+Gi_d0 Sl_nx Yl_k0 Vz_e Gi_d1 Ve00 Ve01 Ve02 Sl_st Yl_k1 Ve03 Vq_e0 Ve12 Ve13 Ve11 Ve10 Vq_k0 Yl_x0 Vc_o1 Gz_stg Gs_nx Yl_x1
+Gz_stb Sg10_0 Vc_o2 Vc_o3 Gs_ka Gsig0 Vc_o0 Vq_e1 Yl_u Vq_k1 Vc_o4 Yga0 Yga1 Vg20_0 Sg30_0 Gi_d2 Vqs0_0 Gs_kb Sg00_0 Sg01_0
+Vqn0 Tms30_0 Tmn000_0 Tms10_0 Gsig Tmn020_0 Gi_rep Sg11_0 Gi_c0 Gi_c1 Vg31_0 Tms20_0 Sg21_0 Vc_eye Aa_nx Vqs1_0 Tmn010_0
+Tms11_0 Gi_c2 Vqn1 Yl_wc Gi_c3 Gz_zz Yl_ws Sev10_0 Sev20_0 Tmn030_0 Tms00_0 Tms31_0 Vc_rep Vc_t Vc_l0 Sev30_0 Tms01_0 Tmn011_0
+Tms21_0 Tmn021_0 Vq_u Sev00_0 Vc_l1 Vp_uq Sev11_0 Tmn001_0 Sev21_0 Vqv0_0 Gz_pw Sev01_0 Tmn031_0 Gs_uq Sev31_0 Vc_w0 Sp_up
+Gs_up Ygb0 Tmu0_0 Vqv1_0 Vc_l2 Vsl0_0 Tmu1_0 Se22 Se21 Aa_k1p Se20 Vsl1_0 Vzz0_0 Tml30_0 Aa_k1q Tml10_0 Vzz1_0 Tml00_0 Se23
+Vtb0_0 Gz_w2 Vta0_0 Tml20_0 Ygb1 Ser30_0 Ser10_0 Ser00_0 Ser20_0 Tml11_0 Aa_k2q Vta1_0 Tml21_0 Vpw0_0 Aa_k2p Tml31_0 Vtb1_0
+Vq_e2 Aa_u1 Vpw1_0 Vof0_0 Vqs0_1 Tml01_0 Ser11_0 Tms20_1 Yl_n2 Ser31_0 Ser21_0 Spp10_1 Tms10_1 Yl_v Vof1_0 Vpq10_1 Tms00_1
+Vpq00_1 Gs_uq2 Gs_up2 Vpq01_1 Tms30_1 Tmn200_1 Spp00_1 Ser01_0 Tmn230_1 Vqs1_1 Spp01_1 Tmn220_1 Spp11_1 Tmn120_1 Vpq11_1
+Tmn130_1 Tmn110_1 Sev20_1 Vev30_1 Tmn100_1 Vc_w1 Tmn210_1 Tmn131_1 Sev10_1 Tms31_1 Tmn111_1 Tmn211_1 Tms21_1 Tmn231_1 Sev00_1
+Tmn221_1 Tms11_1 Vqv0_1 Tmn121_1 Tmn101_1 Tmu0_1 Tmn201_1 Tms01_1 Vc_f0 Vq_v Tml10_1 Vsl0_1 Vc_f1 Tml20_1 Vzz0_1 Sev31_1
+Tml00_1 Sev11_1 Tml30_1 Aa_u2 Yw20 Sev21_1 Sev01_1 Vqv1_1 Vtb0_1 Ser10_1 Ser20_1 Ser00_1 Vta0_1 Tmu1_1 Ser30_1 Tml11_1 Tml31_1
+Tml21_1 Ser11_1 Vsl1_1 Vpw0_1 Vqs0_2 Vof0_1 Vzz1_1 Tml01_1 Vpq10_2 Ser21_1 Tms20_2 Ser31_1 Spp10_2 Tms00_2 Tms10_2 Tms30_2
+Tmn200_2 Vpq00_2 Tmn230_2 Spp00_2 Vtb1_1 Tmn210_2 Tmn130_2 Vta1_1 Vpw1_1 Tmn110_2 Ser01_1 Sev30_2 Vqs1_2 Tmn220_2 Tmn100_2
+Tmn120_2 Yw21 Tms01_2 Vof1_1 Sev10_2 Tms21_2 Tms11_2 Spp01_2 Spp11_2 Vpq01_2 Vpq11_2 Tms31_2 Vev20_2 Tmn131_2 Tmn121_2
+Tmn101_2 Tmn201_2 Tmn231_2 Sev00_2 Vqv0_2 Sev01_2 Tmn221_2 Tmn111_2 Sev21_2 Tmn211_2 Sev11_2 Vev31_2 Tmu0_2 Vsl0_2 Tml30_2
+Tml20_2 Ser30_2 Tml10_2 Vqv1_2 Tml00_2 Vbd0_2 Ser20_2 Tmu1_2 Tml21_2 Ser10_2 Ser00_2 Tml31_2 Vsl1_2 Tml11_2 Tml01_2 Ser21_2
+Vqs0_3 Yo_c0 Ser31_2 Ver11_2 Ser01_2 Vpl0_2 Tmy0 Sey0 Vqs1_3 Yo_y0 Vbd1_2 Vpl1_2 Yo_c1 So_s0 Tmy1 Sey1 So_y1 Yo_s3 Yo_s2
+So_s1 Yo_pl
+"""
+
+
+def mask_of(engines):
+    m = 0
+    for e in engines:
+        m |= 1 << e
+    return m
+
+
+def u8(v):
+    return v.bitcast(dt.uint8)
+
+
+def u32(v):
+    return v.bitcast(dt.uint32)
+
+
+def build_ops():
+    ops = []
+    at = {"chunk": None}
+
+    def op(name, q, c, deps, fn, grp=None, inc=1, after=(), acc=None, fixed=False):
+        ops.append({"name": name, "q": q, "cost": c, "deps": list(deps), "fn": fn, "grp": grp or (name, 0), "inc": inc,
+                    "after": list(after), "acc": acc, "fixed": fixed, "chunk": at["chunk"]})
+
+    def dma(name, q, deps, out, src, rows, size, grp=None, fixed=True):
+        op(name, q, ("dma", (rows, size, 16)), deps, lambda q_, e, T, C: e.dma_start(out(T), src(T)), grp=grp, inc=16, fixed=fixed)
+
+    def scaled(out, src, by):
+        def fn(q_, e, T, C):
+            if q_ == "V":
+                return e.tensor_scalar(out(T), src(T), by, None, ALU.mult)
+            return e.activation(out(T), src(T), ACT.Copy, scale=by)
+        return fn
+
+    def moved(out, src):
+        def fn(q_, e, T, C):
+            if q_ == "V":
+                return e.tensor_copy(out(T), src(T))
+            return e.activation(out(T), src(T), ACT.Copy)
+        return fn
+
+    def quant(name, deps, cq, cp, a, n, tile, grp=None, src=None):
+        b = a if src is None else src
+        op(name, "V", ("q", n), deps,
+           lambda q_, e, T, C: e.quantize_mx(T[cq][:, a:a + n], T[cp][:, a:a + n], T[tile][:, 4 * b:4 * (b + n)]), grp=grp)
+
+    def mm(name, deps, bank, wq, wp, wa, xq, xp, xa, grp, acc=None):
+        def fn(q_, e, T, C):
+            first, last = C["acc"].get(name, (True, True))
+            return e.matmul_mx(T.ps[:, 512 * bank:512 * bank + CH], T[wq][:, wa:wa + 128], T[wp][:, wa:wa + 128],
+                               T[xq][:, xa:xa + CH], T[xp][:, xa:xa + CH], first, last)
+        op(name, "T", ("mm", CH), deps, fn, grp=grp, acc=acc)
+
+    def stage(name, deps, src):
+        for b in range(2):
+            dma("%s%d" % (name, b), "Y", deps, lambda T, b=b: T.stg[b:128:16, 1 - b:1 - b + 2 * P], src, 16, 28672, grp=(name, 0))
+
+    dma("l_nx", "S", [], lambda T: T.nd0[:], lambda T: T.nx[:], 16, 28672)
+    dma("l_st", "S", [], lambda T: T.sti[:], lambda T: T.st[:], 128, 12288)
+    for h in range(2):
+        dma("l_k%d" % h, "Y", [], lambda T, h=h: T.kin[:, 4 * HALF * h:4 * HALF * (h + 1)],
+            lambda T, h=h: T.k[:, 4 * HALF * h:4 * HALF * (h + 1)], 128, 1024 * HALF)
+    for c in range(NCH):
+        dma("l_x%d" % c, "Y", [], lambda T, c=c: T.xin[:, 4 * CH * c:4 * CH * (c + 1)], lambda T, c=c: T.x[:, 4 * CH * c:4 * CH * (c + 1)],
+            128, 1024 * CH)
+    dma("l_u", "Y", ["sig0"], lambda T: T.uin[:], lambda T: T.u[:], 128, 131072)
+    stage("ga", ["z_stg"], lambda T: T.nx[:])
+    dma("l_wc", "Y", ["sig"], lambda T: u8(T.wq[:]), lambda T: T.wc[:], 128, 262144)
+    dma("l_ws", "Y", [], lambda T: T.wp[:], lambda T: T.ws[:], 128, 65536)
+    stage("gb", ["a_nx", "c_w0"], lambda T: T.nd1[:])
+    dma("l_n2", "Y", ["a_nx"], lambda T: T.nxi[:], lambda T: T.nd2[:], 128, 28672)
+    dma("l_v", "Y", [], lambda T: T.vin[:], lambda T: T.v[:], 128, 131072)
+    for b in range(2):
+        dma("w2%d" % b, "Y", ["c_f0", "z_w2"], lambda T, b=b: T.win2[0:128:16, P * b:P * (b + 1)],
+            lambda T, b=b: T.nxf[:, SEG * b:SEG * (b + 1)], 128, 14336, grp=("w2", 0))
+
+    def iota(name, out, pat, base, cm, n, small=True, grp=None):
+        if small:
+            fn = lambda q_, e, T, C: e.iota(out(T), pat, base, cm, allow_small_or_imprecise_dtypes=True)
+        else:
+            fn = lambda q_, e, T, C: e.iota(out(T), pat, base, cm)
+        op(name, "G", ("iota", n), [], fn, grp=grp, fixed=True)
+
+    def remote(name, deps, fn, rows, size, eng):
+        op(name, "G", ("call", (rows, size, eng)), deps, fn, grp=("sent", 0), inc=None, fixed=True)
+
+    def signal(name):
+        op(name, "G", ("el", 0), [], lambda q_, e, T, C: e.sem_inc(T.sem[name], 1), inc=None, fixed=True)
+
+    def xf(T, C, key, j, src, dst):
+        who, engines = C["use"][key][j]
+        rid, pid = C["addr"][who]
+        return RemoteDMATransfer(dst_ids=[DstId(rid=rid, pnc=pid)], dma_engine_mask=mask_of(engines), remote_sem=T.sem[key], src=src, dst=dst)
+
+    def direct(key, src, dst):
+        def fn(q_, e, T, C):
+            who, engines = C["use"][key][0]
+            rid, pid = C["addr"][who]
+            return e.remote_dma(dst(T), src(T), T.sem[key], T.sem.sent, pid, rid, mask_of(engines))
+        return fn
+
+    rest = 2 * P + 4 - CUT
+    iota("i_d0", lambda T: T.dia[:, 0:128], [[1, 128]], 0, -1, 128)
+    iota("i_d1", lambda T: T.dia[:, 128:256], [[32, 4], [16 + FAR, 2], [1, 16]], 0, -1, 128)
+    iota("z_stg", lambda T: T.stg[:, 0:CUT], [[0, CUT]], 0, 0, CUT, small=False, grp=("z_stg", 0))
+    remote("s_nx", ["l_nx"], lambda q_, e, T, C: e.remote_dma_fused(
+        [xf(T, C, "hnx", j, T.nd0[j], T.hnx[j % 2 if j >= 2 else 0]) for j in range(4)], local_sem=T.sem.sent), 16, 28672, 16)
+    iota("z_stb", lambda T: T.stg[:, CUT:CUT + rest], [[0, rest]], 0, 0, rest, small=False, grp=("z_stg", 0))
+    remote("s_ka", ["q_k0"], lambda q_, e, T, C: e.remote_dma_fused(
+        [xf(T, C, "hka", j, u8(T.kq[:, QUART * j:QUART * (j + 1)]), u8(T.hq[:, 0:QUART])) for j in range(2)],
+        local_sem=T.sem.sent), 256, 1024 * QUART, 16)
+    signal("sig0")
+    iota("i_d2", lambda T: T.dia[:, 256:384], [[32, 4], [16 - FAR, 2], [1, 16]], FAR, -1, 128)
+    remote("s_kb", ["q_k1"], lambda q_, e, T, C: e.remote_dma_fused(
+        [xf(T, C, "hkb", j, u8(T.kq[:, HALF + QUART * j:HALF + QUART * (j + 1)]), u8(T.hq[:, QUART:HALF])) for j in range(2)]
+        + [xf(T, C, "hkb", 2, T.kp[:], T.hp[:])], local_sem=T.sem.sent), 384, 1536 * QUART, 14)
+    signal("sig")
+    iota("i_rep", lambda T: T.rep[:], [[16, 8]], 0, 0, 8, small=False)
+    iota("i_c0", lambda T: T.cst[:, 0:16], [[2, 8], [2 + 2 * NB, 2]], 0, 0, 16, grp=("i_c", 0))
+    iota("i_c1", lambda T: T.cst[:, 16:32], [[2, 8], [-2 * NB, 2]], 2 * NB, 0, 16, grp=("i_c", 0))
+    iota("i_c2", lambda T: T.cst[:, 32:64], [[1, 2], [0, 16]], 0, 0, 32, grp=("i_c", 0))
+    iota("i_c3", lambda T: T.cst[:, 64:96], [[0, 16], [1, 2]], 0, 0, 32, grp=("i_c", 0))
+    iota("z_zz", lambda T: T.zz[:], [[0, ZW * NCH]], 0, 0, ZW * NCH)
+    iota("z_pw", lambda T: T.pw[:], [[0, 32 * NCH]], 0, 0, 32 * NCH)
+    remote("s_uq", ["p_uq"], direct("huq", lambda T: u8(T.u0q[:]), lambda T: u8(T.huq[:])), 128, 65536, 12)
+    remote("s_up", ["p_up"], direct("hup", lambda T: T.u0p[:], lambda T: T.hup[:]), 128, 16384, 12)
+    iota("z_w2", lambda T: T.win2[:], [[0, 2 * P]], 0, 0, 2 * P)
+    remote("s_uq2", ["a_k1q", "a_k1p"], direct("a_u2", lambda T: u8(T.u0q[:]), lambda T: u8(T.u2q[:])), 128, 65536, 8)
+    remote("s_up2", [], direct("a_u2", lambda T: T.u0p[:], lambda T: T.u2p[:]), 128, 16384, 8)
+
+    for name, after, n in (("a_nx", "s_nx", 1.0), ("a_k1q", "s_kb", 1.0), ("a_k1p", "s_kb", 1.0), ("a_u1", "s_up", 1.0),
+                           ("a_k2q", "s_kb", 1.8), ("a_k2p", "s_up", 1.4), ("a_u2", "s_up2", 0.1)):
+        op(name, "A", ("arr", n), [], None, inc=None, after=[after])
+
+    op("z_e", "V", ("el", 1024), [], lambda q_, e, T, C: e.memset(T.et[:], 0.0))
+    op("c_eye", "V", ("el", 64), ["i_d2"], lambda q_, e, T, C: e.tensor_scalar(T.eye[:], T.dia[:, 256:384], 0.0, None, ALU.is_equal))
+    op("c_t", "V", ("el", 96), ["i_c0"], lambda q_, e, T, C: e.transpose(T.cstt[:], T.cst[:]))
+    op("c_l0", "V", ("el", 1), ["c_t"], lambda q_, e, T, C: e.tensor_copy(T.wrap[:, 0:1], T.cstt[:, 0:1]), grp=("c_l", 0))
+    op("c_l1", "V", ("el", 1), ["c_t"],
+       lambda q_, e, T, C: e.tensor_scalar(T.wrap[:, 1:2], T.cstt[:, 0:1], 1.0, None, ALU.add), grp=("c_l", 0))
+    op("c_l2", "V", ("el", 1), ["c_t"],
+       lambda q_, e, T, C: e.tensor_scalar(T.wrap[:, 2:3], T.cstt[:, 0:1], T.cstt[:, 32:33], None, ALU.add), grp=("c_l", 0))
+    op("c_rep", "V", ("el", 8), ["i_rep"], lambda q_, e, T, C: e.tensor_copy(T.repo[:], T.rep[:]))
+    for s in range(3):
+        for b in range(4):
+            out = lambda T, b=b: T.et[:, 513 * b:512 * (b + 1):4]
+            if s < 2:
+                op("e%d%d" % (s, b), "V", ("el", 64), ["i_d%d" % s, "z_e" if s == 0 else "q_e0"], lambda q_, e, T, C, out=out, s=s: e.tensor_scalar(
+                    out(T), T.dia[:, 128 * s:128 * (s + 1)], 0.0, None, ALU.is_equal), grp=("e_w", s))
+            else:
+                op("e%d%d" % (s, b), "S", ("el", 128), ["q_e1", "c_eye"], moved(out, lambda T: T.eye[:]), grp=("e_w", s))
+        quant("q_e%d" % s, ["e%d0" % s], "eq", "ep", 512 * s, 512, "et", grp=("q_e", s), src=0)
+
+    for b in range(2):
+        quant("q_k%d" % b, ["l_k%d" % b], "kq", "kp", HALF * b, HALF, "kin")
+        op("c_w%d" % b, "V", ("el", P), ["ga0" if b == 0 else "gb0"], lambda q_, e, T, C, b=b: e.tensor_scalar(
+            T["win%d" % b][:], T.stg[:, 1:2 * P + 1:2], float(-HALF), None, ALU.add))
+    W = TOK // 16
+    for t in range(4):
+        op("c_o%d" % t, "V", ("el", W), ["l_st"], lambda q_, e, T, C, t=t: e.tensor_scalar(
+            T.o0[:, W * t:W * (t + 1)], T.sti[:], 4.0, float(t), ALU.mult, ALU.add))
+    op("c_o4", "V", ("el", W), ["l_st"], lambda q_, e, T, C: e.tensor_copy(T.o0[:, 4 * W:5 * W], T.sti[:]))
+    quant("q_u", ["l_u"], "uq", "up", 0, 128, "uin")
+    op("p_uq", "V", ("g", 128), ["q_u", "c_rep"],
+       lambda q_, e, T, C: e.tensor_copy(u32(T.u0q[:]), u32(T.uq[:]).indirect(T.repo[:])))
+    op("p_up", "SV", ("g", 128), ["q_u", "c_rep"], moved(lambda T: T.u0p[:], lambda T: T.up[:].indirect(T.repo[:])))
+    quant("q_v", ["l_v"], "vq", "vp", 0, 128, "vin")
+    op("c_f0", "V", ("el", SEG), ["l_n2"],
+       lambda q_, e, T, C: e.tensor_copy(T.nxf[:, 0:SEG], T.nxi[:, 0:2 * SEG:2]), grp=("c_f", 0))
+    op("c_f1", "V", ("el", SEG), ["l_n2"],
+       lambda q_, e, T, C: e.tensor_tensor(T.nxf[:, SEG:2 * SEG], T.nxi[:, 1:2 * SEG:2], T.nxi[:, 0:2 * SEG:2], ALU.subtract), grp=("c_f", 0))
+
+    for c in range(NCH):
+        a = CH * c
+        at["chunk"] = c
+        quant("qs%d_0" % c, ["l_x%d" % c], "sq", "sp", a, CH, "xin", grp=("qs%d" % c, 0))
+        for t in range(HOPS):
+            n = "%d_%d" % (c, t)
+            if t == 0:
+                for b in range(4):
+                    op("g%d%s" % (b, n), "SV", ("g", CH), ["l_k0", "l_k1", "c_o%d" % b], moved(
+                        lambda T, b=b, a=a: T.nt[:, 4 * a + b:4 * (a + CH):4],
+                        lambda T, b=b, c=c: T.kin[:].indirect(T.o0[:, W * b + NL * c:W * b + NL * (c + 1)])), grp=("g%d" % c, 0))
+                quant("qn%d" % c, ["g0" + n], "nq", "npl", a, CH, "nt")
+                nodes = [(0, "nq", "npl", a, ["qn%d" % c])]
+                nat = lambda T, c=c: T.o0[:, 4 * W + NL * c:4 * W + NL * (c + 1)]
+                natdep = "c_o4"
+            else:
+                nodes = []
+                natdep = "of%d_%d" % (c, t - 1)
+                for s in range(2):
+                    lst = lambda T, c=c, s=s: T.off[:, 48 * c + 16 * s:48 * c + 16 * s + NL]
+                    to = TOK * s + a
+                    op("pq%d%s" % (s, n), "V", ("g", CH), [natdep, "a_k%dq" % t], lambda q_, e, T, C, lst=lst, to=to, t=t: e.tensor_copy(
+                        u32(T.pq[:, to:to + CH]), u32(T["k%dq" % t][:]).indirect(lst(T))), grp=("pk%d%d" % (s, c), t))
+                    op("pp%d%s" % (s, n), "SV", ("g", CH), [natdep, "a_k%dp" % t], moved(
+                        lambda T, to=to: T.ppl[:, to:to + CH],
+                        lambda T, lst=lst, t=t: T["k%dp" % t][:].indirect(lst(T))), grp=("pk%d%d" % (s, c), t))
+                    nodes.append((1 + s, "pq", "ppl", to, ["pq%d%s" % (s, n)]))
+                nat = lambda T, c=c: T.off[:, 48 * c + 32:48 * c + 32 + NL]
+            for b in range(4):
+                bank, grp = 4 * c + b, ("bk%d" % (4 * c + b), 2 * t)
+                free = [] if t == 0 else ["er%d%d_%d" % (b, c, t - 1)]
+                mm("ms%d%s" % (b, n), ["qs" + n, "q_e0"], bank, "eq", "ep", 128 * b, "sq", "sp", a, grp, acc=grp)
+                for s, xq, xp, xa, deps in nodes:
+                    mm("mn%d%d%s" % (s, b, n), deps + free + ["q_e%d" % s], bank, "eq", "ep", 512 * s + 128 * b, xq, xp, xa, grp, acc=grp)
+                op("ev%d%s" % (b, n), "SV", ("el", CH), ["ms%d%s" % (b, n)], scaled(
+                    lambda T, b=b, a=a: T.vt[:, 4 * a + b:4 * (a + CH):4],
+                    lambda T, bank=bank: T.ps[:, 512 * bank:512 * bank + CH], 0.5), grp=("ev%d" % c, t))
+            quant("qv" + n, ["ev0" + n], "bq", "bp", a, CH, "vt", grp=("qv%d" % c, t))
+            udeps = ["p_uq", "p_up"] if t == 0 else ["a_u%d" % t]
+            mm("mu" + n, ["qv" + n] + udeps, 4 * c, "u%dq" % t, "u%dp" % t, 0, "bq", "bp", a, ("mu%d" % c, t))
+            score = lambda T, c=c: T.ps[:, 2048 * c:2048 * c + CH]
+            sel = lambda T, a=a: T.sel[:, a:a + CH]
+            if t < HOPS - 1:
+                op("sl" + n, "V", ("el", CH), ["mu" + n, "c_t"], lambda q_, e, T, C, score=score, sel=sel: e.tensor_scalar(
+                    sel(T), score(T), 0.0, T.cstt[:, 64:65], ALU.is_gt, ALU.is_equal), grp=("sl%d" % c, t))
+                z, y = ZW * c, TW * c
+                op("zz" + n, "V", ("g", CH), ["sl" + n, "c_w%d" % t, natdep, "z_zz"], lambda q_, e, T, C, z=z, t=t, nat=nat, sel=sel: e.tensor_tensor(
+                    T.zz[:, z + 16:z + 16 + CH], T["win%d" % t][:].indirect(nat(T)), sel(T), ALU.mult), grp=("zz%d" % c, t))
+                op("ta" + n, "V", ("el", CH // 2), ["zz" + n], lambda q_, e, T, C, z=z, y=y: e.transpose(
+                    T.tt[:, y:y + CH], T.zz[:, z + 16:z + 16 + CH]), grp=("tt%d" % c, t))
+                op("tb" + n, "V", ("el", ZW // 2), ["zz" + n], lambda q_, e, T, C, z=z, y=y: e.transpose(
+                    T.tt[:, y + CH:y + TW], T.zz[:, z:z + ZW]), grp=("tt%d" % c, t))
+                op("pw" + n, "V", ("el", 52), ["ta" + n, "z_pw"], lambda q_, e, T, C, c=c, y=y: e.tensor_tensor(
+                    T.pw[:, 32 * c:32 * c + TW // 16], T.tt[:, y:y + TW:16], T.tt[:, y + 1:y + TW:16], ALU.add), grp=("pw%d" % c, t))
+                op("of" + n, "V", ("g", 48), ["pw" + n, "c_l0"], lambda q_, e, T, C, c=c: e.tensor_scalar(
+                    T.off[:, 48 * c:48 * (c + 1)], T.pw[:, 32 * c:32 * (c + 1)].indirect(T.wrap[:, 0:3]), float(HALF), None, ALU.add),
+                   grp=("of%d" % c, t))
+            else:
+                op("sl" + n, "V", ("el", CH), ["mu" + n], lambda q_, e, T, C, score=score, sel=sel: e.tensor_scalar(
+                    sel(T), score(T), 0.0, None, ALU.is_gt), grp=("sl%d" % c, t))
+                op("bd" + n, "V", ("g", CH), ["sl" + n, "w20", natdep], lambda q_, e, T, C, a=a, nat=nat, sel=sel: e.tensor_tensor(
+                    T.bd[:, a:a + CH], T.win2[:, P:2 * P].indirect(nat(T)), sel(T), ALU.mult))
+                op("pl" + n, "V", ("g", CH), ["bd" + n], lambda q_, e, T, C, a=a, nat=nat: e.tensor_tensor(
+                    T.plb[:, a:a + CH], T.win2[:, 0:P].indirect(nat(T)), T.bd[:, a:a + CH], ALU.add))
+            for b in range(4):
+                bank = 4 * c + b
+                mm("ml%d%s" % (b, n), ["qv" + n, "l_wc", "l_ws"] + (["sl" + n] if b == 0 else []), bank, "wq", "wp", 128 * b,
+                   "bq", "bp", a, ("bk%d" % bank, 2 * t + 1))
+                op("er%d%s" % (b, n), "SV", ("el", CH), ["ml%d%s" % (b, n)], scaled(
+                    lambda T, b=b, a=a: T.rt[:, 4 * a + b:4 * (a + CH):4],
+                    lambda T, bank=bank: T.ps[:, 512 * bank:512 * bank + CH], 0.03125), grp=("er%d" % c, t))
+            quant("qs%d_%d" % (c, t + 1), ["er0" + n], "sq", "sp", a, CH, "rt", grp=("qs%d" % c, t + 1))
+        last = "qs%d_%d" % (c, HOPS)
+        bank = 4 * c + 1
+        mm("my%d" % c, [last, "q_v"], bank, "vq", "vp", 0, "sq", "sp", a, ("bk%d" % bank, 2 * HOPS))
+        op("ey%d" % c, "SV", ("el", CH), ["my%d" % c], moved(
+            lambda T, a=a: T.yb[:, a:a + CH], lambda T, bank=bank: T.ps[:, 512 * bank:512 * bank + CH]))
+    at["chunk"] = None
+
+    fin = ["qs%d_%d" % (c, HOPS) for c in range(NCH)]
+    for c in range(NCH):
+        q = "Y" if c < NCH - 1 else "YS"
+        dma("o_c%d" % c, q, [fin[c]], lambda T, c=c: T.oc[:, 4 * CH * c:4 * CH * (c + 1)], lambda T, c=c: u8(T.sq[:, CH * c:CH * (c + 1)]),
+            128, 512 * CH, grp=("out", 0), fixed=False)
+        dma("o_y%d" % c, q, ["ey%d" % c], lambda T, c=c: T.y[:, CH * c:CH * (c + 1)], lambda T, c=c: T.yb[:, CH * c:CH * (c + 1)],
+            128, 512 * CH, grp=("out", 0), fixed=False)
+    dma("o_pl", "Y", ["pl%d_%d" % (c, HOPS - 1) for c in range(NCH)], lambda T: T.pl[:], lambda T: T.plb[0:128:16, :],
+        16, 12288, grp=("out", 0), fixed=False)
+    for k in range(4):
+        dma("o_s%d" % k, "YS", fin, lambda T, k=k: T.osc[4 * k:4 * k + 4, :], lambda T, k=k: T.sp[32 * k:32 * k + 4, :],
+            16, 1536, grp=("out", 0), fixed=False)
+    return ops
+
+
+def link(ops):
+    by = {o["name"]: o for o in ops}
+    members, prev = {}, {}
+    for o in ops:
+        members.setdefault(o["grp"], []).append(o["name"])
+    for o in ops:
+        o["need"] = sorted(set(m for d in o["deps"] for m in members[by[d]["grp"]]))
+        o["before"] = [prev[q] for q in o["q"] if q in prev and (o["fixed"] or o["cost"][0] == "dma")]
+        if o["fixed"]:
+            prev[o["q"]] = o["name"]
+    return by, members
+
+
+def arrange(plan):
+    ops = build_ops()
+    by, members = link(ops)
+    order, place = [], {}
+    for word in plan.split():
+        o = by[word[1:]]
+        o["on"] = word[0]
+        place[o["name"]] = len(order)
+        order.append(o)
+    known = {q: set() for q in "VSTYG"}
+    seen, waited = {}, set()
+    for o in order:
+        o["waits"] = []
+        if o["on"] == "A":
+            seen[o["name"]] = set()
+            continue
+        k = known[o["on"]]
+        for d in sorted(o["need"], key=lambda d: -place[d]):
+            if d in k:
+                continue
+            g = by[d]["grp"]
+            o["waits"].append(g)
+            waited.add(g)
+            for m in members[g]:
+                k.add(m)
+                k |= seen[m]
+        seen[o["name"]] = set(k)
+    acc, flags = {}, {}
+    for o in order:
+        if o["acc"]:
+            acc.setdefault(o["acc"], []).append(o["name"])
+        o["raise"] = o["grp"] in waited or o["cost"][0] in ("dma", "call", "arr")
+    for names in acc.values():
+        for i, nm in enumerate(names):
+            flags[nm] = (i == 0, i == len(names) - 1)
+    return order, flags
+
+
+ORDER, FLAGS = arrange(PLAN)
+SEMAPHORES = sorted(set(o["grp"][0] for o in ORDER if o["raise"]) | {"hnx", "hka", "hkb", "huq", "hup"})
+
+
+def roles(T, topo, r):
+    me, one, two = T.cores[r], T.cores[(r - 1) % N], T.cores[(r - 2) % N]
+    own = [c for c in topo.cores_of(me) if c != me and topo.may_write(c, one)]
+    near = [c for c in own if topo.die(c) == topo.die(me)][0]
+    other = [c for c in own if topo.die(c) != topo.die(me)][0]
+    far = [c for c in range(WORLD) if topo.mates(c, one) and topo.may_write(c, one) and topo.may_write(me, c)
+           and topo.may_write(c, two) and topo.die(c) != topo.die(me)][0]
+    return me, [near, other, far], one, two
+
+
+def halves(engines):
+    return engines[:len(engines) // 2], engines[len(engines) // 2:]
+
+
+def rank_sends(topo, me, hands, two):
+    off = topo.engines(me, hands[2])
+    every = topo.engines(me, hands[0])
+    ra, rb = halves([e for e in every if e not in off])
+    oa, ob = halves(off)
+    ea, eb = halves(every)
+    return {"hnx": [(0, ra), (1, rb), (2, oa), (2, ob)], "hka": [(0, ea), (1, eb)], "hkb": [(0, ra), (1, rb), (2, off)],
+            "huq": [(2, off)], "hup": [(2, off)], "a_u2": [(3, topo.engines(me, two))]}
+
+
+def helper_program(g, core, T, topo, r, j):
+    me, hands, one, two = roles(T, topo, r)
+    use = rank_sends(topo, me, hands, two)
+
+    def wait(key):
+        g.wait_ge(T.sem[key], sum(len(e) for who, e in use[key] if who == j))
+
+    eng = topo.engines(core, one)
+    m, n = mask_of(eng), len(eng)
+    a1, a2 = topo.addr(one, core), topo.addr(two, core)
+    d1, d2 = DstId(rid=a1[0], pnc=a1[1]), DstId(rid=a2[0], pnc=a2[1])
+    wait("hnx")
+    parts = [(0, j, eng)] if j < 2 else [(i, 2 + i, halves(eng)[i]) for i in range(2)]
+    g.remote_dma_fused([RemoteDMATransfer(dst_ids=[d1, d2], dma_engine_mask=mask_of(e), remote_sem=T.sem.a_nx, srcs=[T.hnx[i]],
+                                          dsts=[T.nd1[s], T.nd2[s]]) for i, s, e in parts], local_sem=T.sem.sent)
+    if j < 2:
+        cols = [QUART * j, HALF + QUART * j]
+        for i, key in enumerate(("hka", "hkb")):
+            wait(key)
+            g.remote_dma(u8(T.k1q[:, cols[i]:cols[i] + QUART]), u8(T.hq[:, QUART * i:QUART * (i + 1)]), T.sem.a_k1q, T.sem.sent, a1[1], a1[0], m)
+        g.remote_dma_fused([RemoteDMATransfer(
+            dst_ids=[d2], dma_engine_mask=mask_of(halves(eng)[i]), remote_sem=T.sem.a_k2q,
+            src=u8(T.hq[:, QUART * i:QUART * (i + 1)]), dst=u8(T.k2q[:, cols[i]:cols[i] + QUART])) for i in range(2)], local_sem=T.sem.sent)
+        calls = 4
+    else:
+        wait("hkb")
+        g.remote_dma(T.k1p[:], T.hp[:], T.sem.a_k1p, T.sem.sent, a1[1], a1[0], m)
+        wait("huq")
+        g.remote_dma(u8(T.u1q[:]), u8(T.huq[:]), T.sem.a_u1, T.sem.sent, a1[1], a1[0], m)
+        wait("hup")
+        g.remote_dma(T.u1p[:], T.hup[:], T.sem.a_u1, T.sem.sent, a1[1], a1[0], m)
+        g.remote_dma(T.k2p[:], T.hp[:], T.sem.a_k2p, T.sem.sent, a2[1], a2[0], m)
+        calls = 5
+    g.wait_ge(T.sem.sent, calls * n)
+
+
+def rank_program(g, core, T, topo):
+    rank = T.rank_of(core)
+    if rank is None:
+        for r in range(N):
+            hands = roles(T, topo, r)[1]
+            if core in hands:
+                helper_program(g, core, T, topo, r, hands.index(core))
+        return
+    me, hands, one, two = roles(T, topo, rank)
+    use = rank_sends(topo, me, hands, two)
+    C = {"acc": FLAGS, "addr": {j: topo.addr(c, me) for j, c in enumerate(hands + [two])}, "use": use}
+    n1 = [len(topo.engines(c, me)) for c in roles(T, topo, (rank + 1) % N)[1]]
+    n2 = [len(topo.engines(c, me)) for c in roles(T, topo, (rank + 2) % N)[1]]
+    inc = {"a_nx": sum(n1) + sum(n2), "a_k1q": 2 * (n1[0] + n1[1]), "a_k1p": n1[2], "a_u1": 2 * n1[2],
+           "a_k2q": n2[0] + n2[1], "a_k2p": n2[2], "a_u2": 2 * len(topo.engines(T.cores[(rank + 2) % N], me)), "sig0": 1, "sig": 1}
+    for name, key in (("s_nx", "hnx"), ("s_ka", "hka"), ("s_kb", "hkb"), ("s_uq", "huq"), ("s_up", "hup"), ("s_uq2", "a_u2"), ("s_up2", "a_u2")):
+        inc[name] = sum(len(e) for who, e in use[key])
+    per = {}
+    for o in ORDER:
+        if o["raise"]:
+            per[o["grp"]] = per.get(o["grp"], 0) + (o["inc"] or inc[o["name"]])
+    value, total = {}, {}
+    for grp in sorted(per):
+        total[grp[0]] = total.get(grp[0], 0) + per[grp]
+        value[grp] = total[grp[0]]
+    handle = {"V": g.vector, "S": g.scalar, "T": g.tensor, "Y": g.sync, "G": g}
+    most = {}
+    for o in ORDER:
+        if o["on"] == "A":
+            continue
+        e = handle[o["on"]]
+        for grp in o["waits"]:
+            e.wait_ge(T.sem[grp[0]], value[grp])
+            most[grp[0]] = max(most.get(grp[0], 0), value[grp])
+        ins = o["fn"](o["on"], e, T, C)
+        if o["raise"] and o["inc"]:
+            ins.then_inc(T.sem[o["grp"][0]], o["inc"])
+    for name in sorted(total):
+        if most.get(name, 0) < total[name]:
+            g.wait_ge(T.sem[name], total[name])

@@ -2,16 +2,22 @@ from concourse.bass import DstId, RemoteDMATransfer
 from concourse.mybir import dt, AluOpType, ActivationFunctionType
 
 N, TOK, P, HOPS = 8, 384, 448, 3
-WORLD = 256
-CH = 192
+CH = 128
 NCH = TOK // CH
 NL = CH // 16
 NB = CH // 32
-HALF, QUART = P // 2, P // 4
+HALF = P // 2
+KA = 140
+KB = (P - KA) // 2
 SEG = P // 16
 NXW = 2 * P * 8 // 512
-FAR, CUT = 256, 600
 ZW, TW = CH + 32, 2 * CH + 32
+PW = 32
+LC = (3 * NL + 15) // 16
+LW = 16 * LC
+EW = 520
+BANKS = 8
+FINE = True
 CODE, BF, F32, I32, U16, U8 = "float8_e4m3fn_x4", "bfloat16", "float32", "int32", "uint16", "uint8"
 
 SCRATCH = {
@@ -30,47 +36,31 @@ SCRATCH = {
     "nd0": ("dram", [4, 128, NXW], I32), "nd1": ("dram", [4, 128, NXW], I32), "nd2": ("dram", [4, 128, NXW], I32),
     "stg": ("sbuf", [128, 2 * P + 4], I32), "nxf": ("sbuf", [128, 2 * SEG], F32),
     "win0": ("sbuf", [128, P], BF), "win1": ("sbuf", [128, P], BF), "win2": ("sbuf", [128, 2 * P], F32),
-    "dia": ("sbuf", [128, 384], BF), "eye": ("sbuf", [128, 128], BF),
-    "cst": ("sbuf", [128, 96], F32), "cstt": ("sbuf", [128, 96], F32),
-    "rep": ("sbuf", [128, 8], I32), "repo": ("sbuf", [128, 8], U16), "wrap": ("sbuf", [128, 4], U16),
-    "et": ("sbuf", [128, 2048], BF), "eq": ("sbuf", [128, 1536], CODE), "ep": ("sbuf", [128, 1536], U8),
-    "o0": ("sbuf", [128, 5 * TOK // 16], U16), "off": ("sbuf", [128, 48 * NCH], U16),
+    "dia": ("sbuf", [128, 128], BF), "cst": ("sbuf", [128, 96], F32), "cstt": ("sbuf", [128, 96], F32),
+    "lay": ("sbuf", [128, 32 * LC], F32), "layt": ("sbuf", [128, 32 * LC], F32),
+    "rep": ("sbuf", [128, 8], I32), "repo": ("sbuf", [128, 8], U16), "wrap": ("sbuf", [128, LC], U16),
+    "et": ("sbuf", [128, 3 * EW], BF), "eq": ("sbuf", [128, 1536], CODE), "ep": ("sbuf", [128, 1536], U8),
+    "o0": ("sbuf", [128, 5 * TOK // 16], U16), "off": ("sbuf", [128, LW * NCH], U16),
     "nt": ("sbuf", [128, 4 * TOK], BF), "vt": ("sbuf", [128, 4 * TOK], BF), "rt": ("sbuf", [128, 4 * TOK], BF),
     "nq": ("sbuf", [128, TOK], CODE), "npl": ("sbuf", [128, TOK], U8),
     "bq": ("sbuf", [128, TOK], CODE), "bp": ("sbuf", [128, TOK], U8),
     "sq": ("sbuf", [128, TOK], CODE), "sp": ("sbuf", [128, TOK], U8),
     "pq": ("sbuf", [128, 2 * TOK], CODE), "ppl": ("sbuf", [128, 2 * TOK], U8),
     "sel": ("sbuf", [128, TOK], BF), "zz": ("sbuf", [128, ZW * NCH], BF), "tt": ("sbuf", [128, TW * NCH], BF),
-    "pw": ("sbuf", [128, 32 * NCH], F32), "bd": ("sbuf", [128, TOK], F32), "plb": ("sbuf", [128, TOK], F32),
+    "pw": ("sbuf", [128, PW * NCH], F32), "bd": ("sbuf", [128, TOK], F32), "plb": ("sbuf", [128, TOK], F32),
     "yb": ("sbuf", [128, TOK], F32),
-    "hq": ("sbuf", [128, HALF], CODE), "hp": ("sbuf", [128, P], U8),
-    "huq": ("sbuf", [128, 128], CODE), "hup": ("sbuf", [128, 128], U8), "hnx": ("dram", [2, 128, NXW], I32),
-    "ps": ("psum", [128, 4096], F32),
+    "hq": ("sbuf", [128, max(KA, KB)], CODE), "hp": ("sbuf", [128, P], U8),
+    "huq": ("sbuf", [128, 128], CODE), "hup": ("sbuf", [128, 128], U8), "hnx": ("dram", [128, NXW], I32),
+    "ps": ("psum", [128, 512 * BANKS], F32),
 }
 
 ALU, ACT = AluOpType, ActivationFunctionType
 
 PLAN = """
-Gi_d0 Sl_nx Yl_k0 Vz_e Gi_d1 Ve00 Ve01 Ve02 Sl_st Yl_k1 Ve03 Vq_e0 Ve12 Ve13 Ve11 Ve10 Vq_k0 Yl_x0 Vc_o1 Gz_stg Gs_nx Yl_x1
-Gz_stb Sg10_0 Vc_o2 Vc_o3 Gs_ka Gsig0 Vc_o0 Vq_e1 Yl_u Vq_k1 Vc_o4 Yga0 Yga1 Vg20_0 Sg30_0 Gi_d2 Vqs0_0 Gs_kb Sg00_0 Sg01_0
-Vqn0 Tms30_0 Tmn000_0 Tms10_0 Gsig Tmn020_0 Gi_rep Sg11_0 Gi_c0 Gi_c1 Vg31_0 Tms20_0 Sg21_0 Vc_eye Aa_nx Vqs1_0 Tmn010_0
-Tms11_0 Gi_c2 Vqn1 Yl_wc Gi_c3 Gz_zz Yl_ws Sev10_0 Sev20_0 Tmn030_0 Tms00_0 Tms31_0 Vc_rep Vc_t Vc_l0 Sev30_0 Tms01_0 Tmn011_0
-Tms21_0 Tmn021_0 Vq_u Sev00_0 Vc_l1 Vp_uq Sev11_0 Tmn001_0 Sev21_0 Vqv0_0 Gz_pw Sev01_0 Tmn031_0 Gs_uq Sev31_0 Vc_w0 Sp_up
-Gs_up Ygb0 Tmu0_0 Vqv1_0 Vc_l2 Vsl0_0 Tmu1_0 Se22 Se21 Aa_k1p Se20 Vsl1_0 Vzz0_0 Tml30_0 Aa_k1q Tml10_0 Vzz1_0 Tml00_0 Se23
-Vtb0_0 Gz_w2 Vta0_0 Tml20_0 Ygb1 Ser30_0 Ser10_0 Ser00_0 Ser20_0 Tml11_0 Aa_k2q Vta1_0 Tml21_0 Vpw0_0 Aa_k2p Tml31_0 Vtb1_0
-Vq_e2 Aa_u1 Vpw1_0 Vof0_0 Vqs0_1 Tml01_0 Ser11_0 Tms20_1 Yl_n2 Ser31_0 Ser21_0 Spp10_1 Tms10_1 Yl_v Vof1_0 Vpq10_1 Tms00_1
-Vpq00_1 Gs_uq2 Gs_up2 Vpq01_1 Tms30_1 Tmn200_1 Spp00_1 Ser01_0 Tmn230_1 Vqs1_1 Spp01_1 Tmn220_1 Spp11_1 Tmn120_1 Vpq11_1
-Tmn130_1 Tmn110_1 Sev20_1 Vev30_1 Tmn100_1 Vc_w1 Tmn210_1 Tmn131_1 Sev10_1 Tms31_1 Tmn111_1 Tmn211_1 Tms21_1 Tmn231_1 Sev00_1
-Tmn221_1 Tms11_1 Vqv0_1 Tmn121_1 Tmn101_1 Tmu0_1 Tmn201_1 Tms01_1 Vc_f0 Vq_v Tml10_1 Vsl0_1 Vc_f1 Tml20_1 Vzz0_1 Sev31_1
-Tml00_1 Sev11_1 Tml30_1 Aa_u2 Yw20 Sev21_1 Sev01_1 Vqv1_1 Vtb0_1 Ser10_1 Ser20_1 Ser00_1 Vta0_1 Tmu1_1 Ser30_1 Tml11_1 Tml31_1
-Tml21_1 Ser11_1 Vsl1_1 Vpw0_1 Vqs0_2 Vof0_1 Vzz1_1 Tml01_1 Vpq10_2 Ser21_1 Tms20_2 Ser31_1 Spp10_2 Tms00_2 Tms10_2 Tms30_2
-Tmn200_2 Vpq00_2 Tmn230_2 Spp00_2 Vtb1_1 Tmn210_2 Tmn130_2 Vta1_1 Vpw1_1 Tmn110_2 Ser01_1 Sev30_2 Vqs1_2 Tmn220_2 Tmn100_2
-Tmn120_2 Yw21 Tms01_2 Vof1_1 Sev10_2 Tms21_2 Tms11_2 Spp01_2 Spp11_2 Vpq01_2 Vpq11_2 Tms31_2 Vev20_2 Tmn131_2 Tmn121_2
-Tmn101_2 Tmn201_2 Tmn231_2 Sev00_2 Vqv0_2 Sev01_2 Tmn221_2 Tmn111_2 Sev21_2 Tmn211_2 Sev11_2 Vev31_2 Tmu0_2 Vsl0_2 Tml30_2
-Tml20_2 Ser30_2 Tml10_2 Vqv1_2 Tml00_2 Vbd0_2 Ser20_2 Tmu1_2 Tml21_2 Ser10_2 Ser00_2 Tml31_2 Vsl1_2 Tml11_2 Tml01_2 Ser21_2
-Vqs0_3 Yo_c0 Ser31_2 Ver11_2 Ser01_2 Vpl0_2 Tmy0 Sey0 Vqs1_3 Yo_y0 Vbd1_2 Vpl1_2 Yo_c1 So_s0 Tmy1 Sey1 So_y1 Yo_s3 Yo_s2
-So_s1 Yo_pl
+Sl_nx Yl_k0 Gi_d Vz_e Sl_st Yl_k1 Yl_x0 Yl_u Yl_x1 Gi_c0 Ve0 Gi_c1 Gi_c2 Gz_s0 Vq_e03 Vc_t Vq_e00 Vq_e02 Vz_s1 Gs_nx Yga0 Se1 Se2 Sga1 Vc_o1 Vq_e01 Vc_o2 Vc_o3 Vq_k0 Vc_o4 Gi_rep Gs_ka Vc_o0 Vq_e20 Vq_k1 Gs_kb Vg20_0 Vqs0_0 Vg22_0 Vg30_0 Sg00_0 Sg32_0 Sg02_0 Sg12_0 Gs_kp Gsgkp Gi_l0 Gi_l1 Yl_x2 Tms20_0 Tms10_0 Tms30_0 Yl_wc Gi_l2 Yl_ws Sg10_0 Sg01_0 Sg21_0 Sg11_0 Sg31_0 Vc_rep Vq_u Vqs1_0 Vqn0 Vqn2 Vp_uq Vq_e21 Gs_uq Tmn030_0 Tms01_0 Vq_e10 Vq_e13 Tmn010_0 Tmn000_0 Tms00_0 Tms11_0 Tms31_0 Tmn020_0 Tmn002_0 Sp_up Vq_e23 Vqn1 Vq_e12 Sev00_0 Vev30_0 Sev10_0 Sev20_0 Vq_e11 Vq_e22 Gs_up Tmn011_0 Tmn001_0 Gz_zz Sev11_0 Tmn021_0 Tmn031_0 Tmn022_0 Tms21_0 Sev01_0 Aa_nx Sev31_0 Sev21_0 Vqv0_0 Vqs2_0 Vc_w0 Tmu0_0 Tms32_0 Tms22_0 Tms02_0 Tmn012_0 Tmn032_0 Tms12_0 Gi_l3 Vsl0_0 Sev02_0 Sev22_0 Gi_l4 Vqv1_0 Aa_k1q Ygb0 Aa_k1p Ygb1 Gi_l5 Yl_n2 Sev12_0 Yl_v Vzz0_0 Gz_w2 Tmu1_0 Sev32_0 Vc_u Tml00_0 Tml10_0 Vsl1_0 Vtb0_0 Vqv2_0 Ser00_0 Ser10_0 Tmu2_0 Tml20_0 Vzz1_0 Vc_l Vta0_0 Ser20_0 Tml01_0 Tml30_0 Tml11_0 Aa_k2q Aa_u1 Vta1_0 Vsl2_0 Vtb1_0 Vpw0_0 Vzz2_0 Ser30_0 Tml12_0 Tml22_0 Tml32_0 Tml31_0 Vpw1_0 Vof0_0 Ser01_0 Ser11_0 Ser31_0 Aa_u2 Ser22_0 Vqs0_1 Vta2_0 Vof1_0 Spp0_1 Vpq0_1 Tms30_1 Tml02_0 Tml21_0 Tms10_1 Tms20_1 Tms00_1 Aa_k2p Ser21_0 Spp1_1 Vtb2_0 Vpq1_1 Tmn200_1 Tmn100_1 Tmn120_1 Tmn230_1 Tmn220_1 Tmn210_1 Tmn110_1 Vpw2_0 Sev00_1 Ser02_0 Vqs1_1 Sev20_1 Tmn130_1 Tmn131_1 Tmn201_1 Tms11_1 Tmn221_1 Tmn121_1 Tms21_1 Tms01_1 Tms31_1 Vof2_0 Vc_w1 Sev10_1 Sev30_1 Tmn111_1 Tmn101_1 Vqv0_1 Vpq2_1 Tmu0_1 Tmn211_1 Tmn231_1 Spp2_1 Ser32_0 Ser12_0 Sev21_1 Vsl0_1 Vqs2_1 Vc_f1 Tml00_1 Vzz0_1 Sev01_1 Sev31_1 Sev11_1 Tml20_1 Tmn232_1 Tml10_1 Tmn212_1 Tms32_1 Tmn132_1 Tmn222_1 Tmn122_1 Tms12_1 Tmn112_1 Vqv1_1 Vta0_1 Vtb0_1 Tmu1_1 Vq_v Tms02_1 Tms22_1 Tmn102_1 Tmn202_1 Vpw0_1 Ser20_1 Ser10_1 Sev32_1 Ser00_1 Sev12_1 Vsl1_1 Vof0_1 Vc_f0 Sev22_1 Tml30_1 Vzz1_1 Sev02_1 Yw20 Yw21 Tml21_1 Tml11_1 Tml31_1 Ser30_1 Vqv2_1 Vtb1_1 Vta1_1 Vqs0_2 Vpq0_2 Tml02_1 Tmu2_1 Tml01_1 Tml12_1 Tml22_1 Ser11_1 Ser31_1 Spp0_2 Ser01_1 Ser21_1 Vpw1_1 Vsl2_1 Vof1_1 Vqs1_2 Ser02_1 Ser22_1 Tms00_2 Tms10_2 Tml32_1 Ser32_1 Ser12_1 Vzz2_1 Tmn100_2 Tmn200_2 Tms20_2 Tmn230_2 Tmn110_2 Tmn220_2 Tms21_2 Tms30_2 Spp1_2 Tmn210_2 Tms31_2 Tms01_2 Tmn130_2 Tmn120_2 Vpq1_2 Vtb2_1 Vta2_1 Sev10_2 Sev00_2 Sev30_2 Sev20_2 Tmn201_2 Tmn101_2 Tmn221_2 Tmn121_2 Vqs2_2 Vpw2_1 Sev01_2 Vof2_1 Sev21_2 Vqv0_2 Spp2_2 Vpq2_2 Tmn131_2 Tmn111_2 Tmn211_2 Tms02_2 Tmn231_2 Tms22_2 Sev31_2 Tml10_2 Tmu0_2 Vsl0_2 Tml30_2 Tms11_2 Tml00_2 Ser30_2 Vev11_2 Vbd0_2 Ser00_2 Vqv1_2 Tmn222_2 Tmn102_2 Tml20_2 Tmn212_2 Tmn122_2 Ser20_2 Ser10_2 Vpl0_2 Sev22_2 Tmn232_2 Tmn132_2 Tms32_2 Tms12_2 Tmn112_2 Tmn202_2 Vqs0_3 Sev32_2 Tml01_2 Tml31_2 Vev02_2 Sev12_2 Yo_c0 Tml21_2 Tml11_2 Tmy0 Ver31_2 Ser01_2 Vqv2_2 Tmu1_2 Ser21_2 Ver11_2 Sey0 Vsl1_2 Tml22_2 Tml32_2 Vqs1_3 Yo_y0 Tml02_2 Tml12_2 Ser22_2 Vbd1_2 Tmu2_2 Ser32_2 Yo_c1 Tmy1 Ver02_2 Ser12_2 Vsl2_2 Sey1 Vqs2_3 Vbd2_2 Yo_y1 Tmy2 Yo_c2 Yo_s0 Vpl1_2 Sey2 Yo_s1 Vpl2_2 So_y2 Yo_s2 Yo_s3 So_pl
 """
+
+GATE = {"l_x2": ["sgkp"]}
 
 
 def mask_of(engines):
@@ -90,56 +80,56 @@ def u32(v):
 
 def build_ops():
     ops = []
-    at = {"chunk": None}
 
-    def op(name, q, c, deps, fn, grp=None, inc=1, after=(), acc=None, fixed=False):
-        ops.append({"name": name, "q": q, "cost": c, "deps": list(deps), "fn": fn, "grp": grp or (name, 0), "inc": inc,
-                    "after": list(after), "acc": acc, "fixed": fixed, "chunk": at["chunk"]})
+    def op(name, q, c, deps, fn, grp=None, inc=1, acc=None, reads=None):
+        ops.append({"name": name, "q": q, "cost": c, "deps": list(deps) + GATE.get(name, []), "fn": fn, "grp": grp or (name, 0),
+                    "inc": inc, "acc": acc, "reads": reads})
 
-    def dma(name, q, deps, out, src, rows, size, grp=None, fixed=True):
-        op(name, q, ("dma", (rows, size, 16)), deps, lambda q_, e, T, C: e.dma_start(out(T), src(T)), grp=grp, inc=16, fixed=fixed)
+    def dma(name, q, deps, out, src, rows, size, grp=None):
+        op(name, q, ("dma", (rows, size)), deps, lambda q_, e, T, C: e.dma_start(out(T), src(T)), grp=grp, inc=16)
 
-    def scaled(out, src, by):
-        def fn(q_, e, T, C):
-            if q_ == "V":
-                return e.tensor_scalar(out(T), src(T), by, None, ALU.mult)
-            return e.activation(out(T), src(T), ACT.Copy, scale=by)
-        return fn
+    def bank(T, C, key):
+        return T.ps[:, 512 * C["bank"][key]:512 * C["bank"][key] + CH]
+
+    def scaled(q_, e, out, src, by):
+        if q_ == "V":
+            return e.tensor_copy(out, src) if by is None else e.tensor_scalar(out, src, by, None, ALU.mult)
+        return e.activation(out, src, ACT.Copy) if by is None else e.activation(out, src, ACT.Copy, scale=by)
+
+    def evict(name, deps, out, key, by, grp):
+        op(name, "SV", ("el", CH), deps, lambda q_, e, T, C: scaled(q_, e, out(T), bank(T, C, key), by), grp=grp, reads=key)
 
     def moved(out, src):
-        def fn(q_, e, T, C):
-            if q_ == "V":
-                return e.tensor_copy(out(T), src(T))
-            return e.activation(out(T), src(T), ACT.Copy)
-        return fn
+        return lambda q_, e, T, C: scaled(q_, e, out(T), src(T), None)
 
     def quant(name, deps, cq, cp, a, n, tile, grp=None, src=None):
-        b = a if src is None else src
+        b = 4 * a if src is None else src
         op(name, "V", ("q", n), deps,
-           lambda q_, e, T, C: e.quantize_mx(T[cq][:, a:a + n], T[cp][:, a:a + n], T[tile][:, 4 * b:4 * (b + n)]), grp=grp)
+           lambda q_, e, T, C: e.quantize_mx(T[cq][:, a:a + n], T[cp][:, a:a + n], T[tile][:, b:b + 4 * n]), grp=grp)
 
-    def mm(name, deps, bank, wq, wp, wa, xq, xp, xa, grp, acc=None):
+    def mm(name, deps, key, wq, wp, wa, xq, xp, xa):
         def fn(q_, e, T, C):
-            first, last = C["acc"].get(name, (True, True))
-            return e.matmul_mx(T.ps[:, 512 * bank:512 * bank + CH], T[wq][:, wa:wa + 128], T[wp][:, wa:wa + 128],
+            first, last = C["acc"][name]
+            return e.matmul_mx(bank(T, C, key), T[wq][:, wa:wa + 128], T[wp][:, wa:wa + 128],
                                T[xq][:, xa:xa + CH], T[xp][:, xa:xa + CH], first, last)
-        op(name, "T", ("mm", CH), deps, fn, grp=grp, acc=acc)
+        op(name, "T", ("mm", CH), deps, fn, grp=(key, 0), acc=key)
 
     def stage(name, deps, src):
         for b in range(2):
-            dma("%s%d" % (name, b), "Y", deps, lambda T, b=b: T.stg[b:128:16, 1 - b:1 - b + 2 * P], src, 16, 28672, grp=(name, 0))
+            dma("%s%d" % (name, b), "YS", deps, lambda T, b=b: T.stg[b:128:16, 1 - b:1 - b + 2 * P], src, 16, 28672, grp=(name, 0))
 
-    dma("l_nx", "S", [], lambda T: T.nd0[:], lambda T: T.nx[:], 16, 28672)
-    dma("l_st", "S", [], lambda T: T.sti[:], lambda T: T.st[:], 128, 12288)
+    cut = (0, KA, P)
+    dma("l_nx", "YS", [], lambda T: T.nd0[:], lambda T: T.nx[:], 16, 28672)
+    dma("l_st", "YS", [], lambda T: T.sti[:], lambda T: T.st[:], 128, 12288)
     for h in range(2):
-        dma("l_k%d" % h, "Y", [], lambda T, h=h: T.kin[:, 4 * HALF * h:4 * HALF * (h + 1)],
-            lambda T, h=h: T.k[:, 4 * HALF * h:4 * HALF * (h + 1)], 128, 1024 * HALF)
+        dma("l_k%d" % h, "Y", [], lambda T, h=h: T.kin[:, 4 * cut[h]:4 * cut[h + 1]], lambda T, h=h: T.k[:, 4 * cut[h]:4 * cut[h + 1]],
+            128, 1024 * (cut[h + 1] - cut[h]))
     for c in range(NCH):
         dma("l_x%d" % c, "Y", [], lambda T, c=c: T.xin[:, 4 * CH * c:4 * CH * (c + 1)], lambda T, c=c: T.x[:, 4 * CH * c:4 * CH * (c + 1)],
             128, 1024 * CH)
-    dma("l_u", "Y", ["sig0"], lambda T: T.uin[:], lambda T: T.u[:], 128, 131072)
-    stage("ga", ["z_stg"], lambda T: T.nx[:])
-    dma("l_wc", "Y", ["sig"], lambda T: u8(T.wq[:]), lambda T: T.wc[:], 128, 262144)
+    dma("l_u", "Y", [], lambda T: T.uin[:], lambda T: T.u[:], 128, 131072)
+    stage("ga", ["z_s0"], lambda T: T.nx[:])
+    dma("l_wc", "Y", [], lambda T: u8(T.wq[:]), lambda T: T.wc[:], 128, 262144)
     dma("l_ws", "Y", [], lambda T: T.wp[:], lambda T: T.ws[:], 128, 65536)
     stage("gb", ["a_nx", "c_w0"], lambda T: T.nd1[:])
     dma("l_n2", "Y", ["a_nx"], lambda T: T.nxi[:], lambda T: T.nd2[:], 128, 28672)
@@ -153,80 +143,75 @@ def build_ops():
             fn = lambda q_, e, T, C: e.iota(out(T), pat, base, cm, allow_small_or_imprecise_dtypes=True)
         else:
             fn = lambda q_, e, T, C: e.iota(out(T), pat, base, cm)
-        op(name, "G", ("iota", n), [], fn, grp=grp, fixed=True)
+        op(name, "G", ("iota", n), [], fn, grp=grp)
 
-    def remote(name, deps, fn, rows, size, eng):
-        op(name, "G", ("call", (rows, size, eng)), deps, fn, grp=("sent", 0), inc=None, fixed=True)
-
-    def signal(name):
-        op(name, "G", ("el", 0), [], lambda q_, e, T, C: e.sem_inc(T.sem[name], 1), inc=None, fixed=True)
-
-    def xf(T, C, key, j, src, dst):
-        who, engines = C["use"][key][j]
-        rid, pid = C["addr"][who]
-        return RemoteDMATransfer(dst_ids=[DstId(rid=rid, pnc=pid)], dma_engine_mask=mask_of(engines), remote_sem=T.sem[key], src=src, dst=dst)
-
-    def direct(key, src, dst):
+    def zero(name, out, n, narrow=False, small=True, grp=None):
         def fn(q_, e, T, C):
-            who, engines = C["use"][key][0]
-            rid, pid = C["addr"][who]
-            return e.remote_dma(dst(T), src(T), T.sem[key], T.sem.sent, pid, rid, mask_of(engines))
-        return fn
+            if q_ == "V":
+                return e.memset(out(T), 0.0 if small else 0)
+            if small:
+                return e.iota(out(T), [[0, n]], 0, 0, allow_small_or_imprecise_dtypes=True)
+            return e.iota(out(T), [[0, n]], 0, 0)
+        op(name, "GV", ("fill", (n, narrow)), [], fn, grp=grp)
 
-    rest = 2 * P + 4 - CUT
-    iota("i_d0", lambda T: T.dia[:, 0:128], [[1, 128]], 0, -1, 128)
-    iota("i_d1", lambda T: T.dia[:, 128:256], [[32, 4], [16 + FAR, 2], [1, 16]], 0, -1, 128)
-    iota("z_stg", lambda T: T.stg[:, 0:CUT], [[0, CUT]], 0, 0, CUT, small=False, grp=("z_stg", 0))
-    remote("s_nx", ["l_nx"], lambda q_, e, T, C: e.remote_dma_fused(
-        [xf(T, C, "hnx", j, T.nd0[j], T.hnx[j % 2 if j >= 2 else 0]) for j in range(4)], local_sem=T.sem.sent), 16, 28672, 16)
-    iota("z_stb", lambda T: T.stg[:, CUT:CUT + rest], [[0, rest]], 0, 0, rest, small=False, grp=("z_stg", 0))
-    remote("s_ka", ["q_k0"], lambda q_, e, T, C: e.remote_dma_fused(
-        [xf(T, C, "hka", j, u8(T.kq[:, QUART * j:QUART * (j + 1)]), u8(T.hq[:, 0:QUART])) for j in range(2)],
-        local_sem=T.sem.sent), 256, 1024 * QUART, 16)
-    signal("sig0")
-    iota("i_d2", lambda T: T.dia[:, 256:384], [[32, 4], [16 - FAR, 2], [1, 16]], FAR, -1, 128)
-    remote("s_kb", ["q_k1"], lambda q_, e, T, C: e.remote_dma_fused(
-        [xf(T, C, "hkb", j, u8(T.kq[:, HALF + QUART * j:HALF + QUART * (j + 1)]), u8(T.hq[:, QUART:HALF])) for j in range(2)]
-        + [xf(T, C, "hkb", 2, T.kp[:], T.hp[:])], local_sem=T.sem.sent), 384, 1536 * QUART, 14)
-    signal("sig")
+    def remote(name, deps, src, dst, size):
+        def fn(q_, e, T, C):
+            return e.remote_dma_fused([RemoteDMATransfer(
+                dst_ids=[DstId(rid=C["addr"][who][0], pnc=C["addr"][who][1])], dma_engine_mask=mask_of(engines),
+                remote_sem=T.sem["h" + name[2:]], src=src(T, i), dst=dst(T)) for i, (who, engines) in enumerate(C["use"][name])],
+                local_sem=T.sem.sent)
+        op(name, "G", ("call", size), deps, fn, grp=("sent", 0), inc=None)
+
+    iota("i_d", lambda T: T.dia[:], [[1, 128]], 0, -1, 128)
+    for i in range(2):
+        zero("z_s%d" % i, lambda T, i=i: T.stg[:, P * i + 1:P * (i + 1) + 1:2], HALF, small=False, grp=("z_s", 0))
+    remote("s_nx", ["l_nx"], lambda T, i: T.nd0[i], lambda T: T.hnx[:], 28672)
+    remote("s_ka", ["q_k0"], lambda T, i: u8(T.kq[:, 0:KA]), lambda T: u8(T.hq[:, 0:KA]), 512 * KA)
+    remote("s_kb", ["q_k1"], lambda T, i: u8(T.kq[:, KA + KB * i:KA + KB * (i + 1)]), lambda T: u8(T.hq[:, 0:KB]), 1024 * KB)
+    remote("s_kp", ["q_k0", "q_k1"], lambda T, i: T.kp[:], lambda T: T.hp[:], 128 * P)
+    remote("s_uq", ["p_uq"], lambda T, i: u8(T.u0q[:]), lambda T: u8(T.huq[:]), 65536)
+    remote("s_up", ["p_up"], lambda T, i: T.u0p[:], lambda T: T.hup[:], 16384)
+    for name in sorted(set(v[0] for v in GATE.values())):
+        op(name, "G", ("sig", "s_" + name[2:]), [], lambda q_, e, T, C, name=name: e.sem_inc(T.sem[name], 1), inc=None)
     iota("i_rep", lambda T: T.rep[:], [[16, 8]], 0, 0, 8, small=False)
-    iota("i_c0", lambda T: T.cst[:, 0:16], [[2, 8], [2 + 2 * NB, 2]], 0, 0, 16, grp=("i_c", 0))
-    iota("i_c1", lambda T: T.cst[:, 16:32], [[2, 8], [-2 * NB, 2]], 2 * NB, 0, 16, grp=("i_c", 0))
-    iota("i_c2", lambda T: T.cst[:, 32:64], [[1, 2], [0, 16]], 0, 0, 32, grp=("i_c", 0))
-    iota("i_c3", lambda T: T.cst[:, 64:96], [[0, 16], [1, 2]], 0, 0, 32, grp=("i_c", 0))
-    iota("z_zz", lambda T: T.zz[:], [[0, ZW * NCH]], 0, 0, ZW * NCH)
-    iota("z_pw", lambda T: T.pw[:], [[0, 32 * NCH]], 0, 0, 32 * NCH)
-    remote("s_uq", ["p_uq"], direct("huq", lambda T: u8(T.u0q[:]), lambda T: u8(T.huq[:])), 128, 65536, 12)
-    remote("s_up", ["p_up"], direct("hup", lambda T: T.u0p[:], lambda T: T.hup[:]), 128, 16384, 12)
-    iota("z_w2", lambda T: T.win2[:], [[0, 2 * P]], 0, 0, 2 * P)
-    remote("s_uq2", ["a_k1q", "a_k1p"], direct("a_u2", lambda T: u8(T.u0q[:]), lambda T: u8(T.u2q[:])), 128, 65536, 8)
-    remote("s_up2", [], direct("a_u2", lambda T: T.u0p[:], lambda T: T.u2p[:]), 128, 16384, 8)
+    iota("i_c0", lambda T: T.cst[:, 0:32], [[0, 16], [1, 2]], 0, 0, 32, grp=("i_c", 0))
+    iota("i_c1", lambda T: T.cst[:, 32:64], [[-1, 2], [0, 16]], 1, 0, 32, grp=("i_c", 0))
+    iota("i_c2", lambda T: T.cst[:, 64:96], [[1, 2], [0, 16]], 0, 0, 32, grp=("i_c", 0))
+    count = 0
+    for odd in range(2):
+        for e0 in range(3 * NL):
+            s, c = e0 // NL, e0 % NL
+            if e0 % 16 and c:
+                continue
+            n = min(16 - e0 % 16, NL - c)
+            times = (16 - e0 % 16) // n if e0 + n == 3 * NL else 1
+            at = 32 * (e0 // 16) + 16 * odd + e0 % 16
+            iota("i_l%d" % count, lambda T, at=at, w=n * times: T.lay[:, at:at + w],
+                 [[0, times], [2, n // 2], [-2 * NB if odd else 2 * NB + 2, 2]], c + (s if s < 2 else odd) + 2 * NB * odd, 0, n * times,
+                 grp=("i_l", 0))
+            count += 1
+    zero("z_zz", lambda T: T.zz[:], ZW * NCH, narrow=True)
+    zero("z_w2", lambda T: T.win2[:], 2 * P)
 
-    for name, after, n in (("a_nx", "s_nx", 1.0), ("a_k1q", "s_kb", 1.0), ("a_k1p", "s_kb", 1.0), ("a_u1", "s_up", 1.0),
-                           ("a_k2q", "s_kb", 1.8), ("a_k2p", "s_up", 1.4), ("a_u2", "s_up2", 0.1)):
-        op(name, "A", ("arr", n), [], None, inc=None, after=[after])
+    for name, after in (("a_nx", []), ("a_k1q", ["s_ka", "s_kb"]), ("a_k1p", ["s_kp"]), ("a_u1", ["s_ka", "s_kp", "s_uq", "s_up"]),
+                        ("a_k2q", ["s_ka", "s_kb", "s_uq"]), ("a_k2p", ["s_kp", "s_up"]), ("a_u2", ["s_ka", "s_kp", "s_uq", "s_up"])):
+        op(name, "A", ("arr", ["s_nx"] + after), [], None, inc=None)
 
-    op("z_e", "V", ("el", 1024), [], lambda q_, e, T, C: e.memset(T.et[:], 0.0))
-    op("c_eye", "V", ("el", 64), ["i_d2"], lambda q_, e, T, C: e.tensor_scalar(T.eye[:], T.dia[:, 256:384], 0.0, None, ALU.is_equal))
+    op("z_e", "V", ("el", EW // 2), [], lambda q_, e, T, C: e.memset(T.et[:, 0:EW], 0.0))
+    op("e0", "V", ("el", 64), ["i_d", "z_e"], lambda q_, e, T, C: e.tensor_scalar(T.et[:, 3:515:4], T.dia[:], 0.0, None, ALU.is_equal))
     op("c_t", "V", ("el", 96), ["i_c0"], lambda q_, e, T, C: e.transpose(T.cstt[:], T.cst[:]))
-    op("c_l0", "V", ("el", 1), ["c_t"], lambda q_, e, T, C: e.tensor_copy(T.wrap[:, 0:1], T.cstt[:, 0:1]), grp=("c_l", 0))
-    op("c_l1", "V", ("el", 1), ["c_t"],
-       lambda q_, e, T, C: e.tensor_scalar(T.wrap[:, 1:2], T.cstt[:, 0:1], 1.0, None, ALU.add), grp=("c_l", 0))
-    op("c_l2", "V", ("el", 1), ["c_t"],
-       lambda q_, e, T, C: e.tensor_scalar(T.wrap[:, 2:3], T.cstt[:, 0:1], T.cstt[:, 32:33], None, ALU.add), grp=("c_l", 0))
+    op("c_u", "V", ("el", 32 * LC), ["i_l0"], lambda q_, e, T, C: e.transpose(T.layt[:], T.lay[:]))
+    op("c_l", "V", ("el", LC), ["c_u"], lambda q_, e, T, C: e.tensor_copy(T.wrap[:], T.layt[:, 0:32 * LC:32]))
     op("c_rep", "V", ("el", 8), ["i_rep"], lambda q_, e, T, C: e.tensor_copy(T.repo[:], T.rep[:]))
     for s in range(3):
+        if s:
+            op("e%d" % s, "SV", ("el2", EW), ["e0", "c_t"], lambda q_, e, T, C, s=s: scaled(
+                q_, e, T.et[:, EW * s:EW * (s + 1)], T.et[:, 0:EW], T.cstt[:, 32 * s:32 * s + 1]))
         for b in range(4):
-            out = lambda T, b=b: T.et[:, 513 * b:512 * (b + 1):4]
-            if s < 2:
-                op("e%d%d" % (s, b), "V", ("el", 64), ["i_d%d" % s, "z_e" if s == 0 else "q_e0"], lambda q_, e, T, C, out=out, s=s: e.tensor_scalar(
-                    out(T), T.dia[:, 128 * s:128 * (s + 1)], 0.0, None, ALU.is_equal), grp=("e_w", s))
-            else:
-                op("e%d%d" % (s, b), "S", ("el", 128), ["q_e1", "c_eye"], moved(out, lambda T: T.eye[:]), grp=("e_w", s))
-        quant("q_e%d" % s, ["e%d0" % s], "eq", "ep", 512 * s, 512, "et", grp=("q_e", s), src=0)
+            quant("q_e%d%d" % (s, b), ["e%d" % s], "eq", "ep", 512 * s + 128 * b, 128, "et", src=EW * s + 3 - b, grp=("q_e%d" % s, 0))
 
     for b in range(2):
-        quant("q_k%d" % b, ["l_k%d" % b], "kq", "kp", HALF * b, HALF, "kin")
+        quant("q_k%d" % b, ["l_k%d" % b], "kq", "kp", cut[b], cut[b + 1] - cut[b], "kin")
         op("c_w%d" % b, "V", ("el", P), ["ga0" if b == 0 else "gb0"], lambda q_, e, T, C, b=b: e.tensor_scalar(
             T["win%d" % b][:], T.stg[:, 1:2 * P + 1:2], float(-HALF), None, ALU.add))
     W = TOK // 16
@@ -241,12 +226,11 @@ def build_ops():
     quant("q_v", ["l_v"], "vq", "vp", 0, 128, "vin")
     op("c_f0", "V", ("el", SEG), ["l_n2"],
        lambda q_, e, T, C: e.tensor_copy(T.nxf[:, 0:SEG], T.nxi[:, 0:2 * SEG:2]), grp=("c_f", 0))
-    op("c_f1", "V", ("el", SEG), ["l_n2"],
+    op("c_f1", "V", ("el", 2 * SEG), ["l_n2"],
        lambda q_, e, T, C: e.tensor_tensor(T.nxf[:, SEG:2 * SEG], T.nxi[:, 1:2 * SEG:2], T.nxi[:, 0:2 * SEG:2], ALU.subtract), grp=("c_f", 0))
 
     for c in range(NCH):
         a = CH * c
-        at["chunk"] = c
         quant("qs%d_0" % c, ["l_x%d" % c], "sq", "sp", a, CH, "xin", grp=("qs%d" % c, 0))
         for t in range(HOPS):
             n = "%d_%d" % (c, t)
@@ -260,35 +244,29 @@ def build_ops():
                 nat = lambda T, c=c: T.o0[:, 4 * W + NL * c:4 * W + NL * (c + 1)]
                 natdep = "c_o4"
             else:
-                nodes = []
                 natdep = "of%d_%d" % (c, t - 1)
-                for s in range(2):
-                    lst = lambda T, c=c, s=s: T.off[:, 48 * c + 16 * s:48 * c + 16 * s + NL]
-                    to = TOK * s + a
-                    op("pq%d%s" % (s, n), "V", ("g", CH), [natdep, "a_k%dq" % t], lambda q_, e, T, C, lst=lst, to=to, t=t: e.tensor_copy(
-                        u32(T.pq[:, to:to + CH]), u32(T["k%dq" % t][:]).indirect(lst(T))), grp=("pk%d%d" % (s, c), t))
-                    op("pp%d%s" % (s, n), "SV", ("g", CH), [natdep, "a_k%dp" % t], moved(
-                        lambda T, to=to: T.ppl[:, to:to + CH],
-                        lambda T, lst=lst, t=t: T["k%dp" % t][:].indirect(lst(T))), grp=("pk%d%d" % (s, c), t))
-                    nodes.append((1 + s, "pq", "ppl", to, ["pq%d%s" % (s, n)]))
-                nat = lambda T, c=c: T.off[:, 48 * c + 32:48 * c + 32 + NL]
+                lst = lambda T, c=c: T.off[:, LW * c:LW * c + 2 * NL]
+                op("pq" + n, "V", ("g", 2 * CH), [natdep, "a_k%dq" % t], lambda q_, e, T, C, lst=lst, a=a, t=t: e.tensor_copy(
+                    u32(T.pq[:, 2 * a:2 * (a + CH)]), u32(T["k%dq" % t][:]).indirect(lst(T))), grp=("pk%d" % c, t))
+                op("pp" + n, "SV", ("g", 2 * CH), [natdep, "a_k%dp" % t], moved(
+                    lambda T, a=a: T.ppl[:, 2 * a:2 * (a + CH)],
+                    lambda T, lst=lst, t=t: T["k%dp" % t][:].indirect(lst(T))), grp=("pk%d" % c, t))
+                nodes = [(1 + s, "pq", "ppl", 2 * a + CH * s, ["pq" + n]) for s in range(2)]
+                nat = lambda T, c=c: T.off[:, LW * c + 2 * NL:LW * c + 3 * NL]
             for b in range(4):
-                bank, grp = 4 * c + b, ("bk%d" % (4 * c + b), 2 * t)
-                free = [] if t == 0 else ["er%d%d_%d" % (b, c, t - 1)]
-                mm("ms%d%s" % (b, n), ["qs" + n, "q_e0"], bank, "eq", "ep", 128 * b, "sq", "sp", a, grp, acc=grp)
+                key = "bl%d%s" % (b, n)
+                mm("ms%d%s" % (b, n), ["qs" + n, "q_e00"], key, "eq", "ep", 128 * b, "sq", "sp", a)
                 for s, xq, xp, xa, deps in nodes:
-                    mm("mn%d%d%s" % (s, b, n), deps + free + ["q_e%d" % s], bank, "eq", "ep", 512 * s + 128 * b, xq, xp, xa, grp, acc=grp)
-                op("ev%d%s" % (b, n), "SV", ("el", CH), ["ms%d%s" % (b, n)], scaled(
-                    lambda T, b=b, a=a: T.vt[:, 4 * a + b:4 * (a + CH):4],
-                    lambda T, bank=bank: T.ps[:, 512 * bank:512 * bank + CH], 0.5), grp=("ev%d" % c, t))
-            quant("qv" + n, ["ev0" + n], "bq", "bp", a, CH, "vt", grp=("qv%d" % c, t))
+                    mm("mn%d%d%s" % (s, b, n), deps + ["q_e%d0" % s], key, "eq", "ep", 512 * s + 128 * b, xq, xp, xa)
+                evict("ev%d%s" % (b, n), ["ms%d%s" % (b, n)], lambda T, b=b, a=a: T.vt[:, 4 * a + b:4 * (a + CH):4], key, 0.5,
+                      None if FINE else ("ev%d" % c, t))
+            quant("qv" + n, ["ev%d%s" % (b, n) for b in range(4)], "bq", "bp", a, CH, "vt", grp=("qv%d" % c, t))
             udeps = ["p_uq", "p_up"] if t == 0 else ["a_u%d" % t]
-            mm("mu" + n, ["qv" + n] + udeps, 4 * c, "u%dq" % t, "u%dp" % t, 0, "bq", "bp", a, ("mu%d" % c, t))
-            score = lambda T, c=c: T.ps[:, 2048 * c:2048 * c + CH]
+            mm("mu" + n, ["qv" + n] + udeps, "mu" + n, "u%dq" % t, "u%dp" % t, 0, "bq", "bp", a)
             sel = lambda T, a=a: T.sel[:, a:a + CH]
             if t < HOPS - 1:
-                op("sl" + n, "V", ("el", CH), ["mu" + n, "c_t"], lambda q_, e, T, C, score=score, sel=sel: e.tensor_scalar(
-                    sel(T), score(T), 0.0, T.cstt[:, 64:65], ALU.is_gt, ALU.is_equal), grp=("sl%d" % c, t))
+                op("sl" + n, "V", ("el", CH), ["mu" + n, "c_t"], lambda q_, e, T, C, n=n, sel=sel: e.tensor_scalar(
+                    sel(T), bank(T, C, "mu" + n), 0.0, T.cstt[:, 0:1], ALU.is_gt, ALU.is_equal), grp=("sl%d" % c, t), reads="mu" + n)
                 z, y = ZW * c, TW * c
                 op("zz" + n, "V", ("g", CH), ["sl" + n, "c_w%d" % t, natdep, "z_zz"], lambda q_, e, T, C, z=z, t=t, nat=nat, sel=sel: e.tensor_tensor(
                     T.zz[:, z + 16:z + 16 + CH], T["win%d" % t][:].indirect(nat(T)), sel(T), ALU.mult), grp=("zz%d" % c, t))
@@ -296,70 +274,75 @@ def build_ops():
                     T.tt[:, y:y + CH], T.zz[:, z + 16:z + 16 + CH]), grp=("tt%d" % c, t))
                 op("tb" + n, "V", ("el", ZW // 2), ["zz" + n], lambda q_, e, T, C, z=z, y=y: e.transpose(
                     T.tt[:, y + CH:y + TW], T.zz[:, z:z + ZW]), grp=("tt%d" % c, t))
-                op("pw" + n, "V", ("el", 52), ["ta" + n, "z_pw"], lambda q_, e, T, C, c=c, y=y: e.tensor_tensor(
-                    T.pw[:, 32 * c:32 * c + TW // 16], T.tt[:, y:y + TW:16], T.tt[:, y + 1:y + TW:16], ALU.add), grp=("pw%d" % c, t))
-                op("of" + n, "V", ("g", 48), ["pw" + n, "c_l0"], lambda q_, e, T, C, c=c: e.tensor_scalar(
-                    T.off[:, 48 * c:48 * (c + 1)], T.pw[:, 32 * c:32 * (c + 1)].indirect(T.wrap[:, 0:3]), float(HALF), None, ALU.add),
+                op("pw" + n, "V", ("el", TW // 8), ["ta" + n], lambda q_, e, T, C, c=c, y=y: e.tensor_tensor(
+                    T.pw[:, PW * c:PW * c + TW // 16], T.tt[:, y:y + TW:16], T.tt[:, y + 1:y + TW:16], ALU.add), grp=("pw%d" % c, t))
+                op("of" + n, "V", ("g", LW), ["pw" + n, "c_l"], lambda q_, e, T, C, c=c: e.tensor_scalar(
+                    T.off[:, LW * c:LW * (c + 1)], T.pw[:, PW * c:PW * c + TW // 16].indirect(T.wrap[:]), float(HALF), None, ALU.add),
                    grp=("of%d" % c, t))
             else:
-                op("sl" + n, "V", ("el", CH), ["mu" + n], lambda q_, e, T, C, score=score, sel=sel: e.tensor_scalar(
-                    sel(T), score(T), 0.0, None, ALU.is_gt), grp=("sl%d" % c, t))
+                op("sl" + n, "V", ("el", CH), ["mu" + n], lambda q_, e, T, C, n=n, sel=sel: e.tensor_scalar(
+                    sel(T), bank(T, C, "mu" + n), 0.0, None, ALU.is_gt), grp=("sl%d" % c, t), reads="mu" + n)
                 op("bd" + n, "V", ("g", CH), ["sl" + n, "w20", natdep], lambda q_, e, T, C, a=a, nat=nat, sel=sel: e.tensor_tensor(
-                    T.bd[:, a:a + CH], T.win2[:, P:2 * P].indirect(nat(T)), sel(T), ALU.mult))
+                    T.bd[:, a:a + CH], T.win2[:, P:2 * P].indirect(nat(T)), sel(T), ALU.mult), grp=("zz%d" % c, t))
                 op("pl" + n, "V", ("g", CH), ["bd" + n], lambda q_, e, T, C, a=a, nat=nat: e.tensor_tensor(
-                    T.plb[:, a:a + CH], T.win2[:, 0:P].indirect(nat(T)), T.bd[:, a:a + CH], ALU.add))
+                    T.plb[:, a:a + CH], T.win2[:, 0:P].indirect(nat(T)), T.bd[:, a:a + CH], ALU.add), grp=("pw%d" % c, t))
             for b in range(4):
-                bank = 4 * c + b
-                mm("ml%d%s" % (b, n), ["qv" + n, "l_wc", "l_ws"] + (["sl" + n] if b == 0 else []), bank, "wq", "wp", 128 * b,
-                   "bq", "bp", a, ("bk%d" % bank, 2 * t + 1))
-                op("er%d%s" % (b, n), "SV", ("el", CH), ["ml%d%s" % (b, n)], scaled(
-                    lambda T, b=b, a=a: T.rt[:, 4 * a + b:4 * (a + CH):4],
-                    lambda T, bank=bank: T.ps[:, 512 * bank:512 * bank + CH], 0.03125), grp=("er%d" % c, t))
-            quant("qs%d_%d" % (c, t + 1), ["er0" + n], "sq", "sp", a, CH, "rt", grp=("qs%d" % c, t + 1))
-        last = "qs%d_%d" % (c, HOPS)
-        bank = 4 * c + 1
-        mm("my%d" % c, [last, "q_v"], bank, "vq", "vp", 0, "sq", "sp", a, ("bk%d" % bank, 2 * HOPS))
-        op("ey%d" % c, "SV", ("el", CH), ["my%d" % c], moved(
-            lambda T, a=a: T.yb[:, a:a + CH], lambda T, bank=bank: T.ps[:, 512 * bank:512 * bank + CH]))
-    at["chunk"] = None
+                key = "ml%d%s" % (b, n)
+                mm(key, ["qv" + n, "l_wc", "l_ws"], key, "wq", "wp", 128 * b, "bq", "bp", a)
+                evict("er%d%s" % (b, n), [key], lambda T, b=b, a=a: T.rt[:, 4 * a + b:4 * (a + CH):4], key, 0.03125,
+                      None if FINE else ("er%d" % c, t))
+            quant("qs%d_%d" % (c, t + 1), ["er%d%s" % (b, n) for b in range(4)], "sq", "sp", a, CH, "rt", grp=("qs%d" % c, t + 1))
+        mm("my%d" % c, ["qs%d_%d" % (c, HOPS), "q_v"], "my%d" % c, "vq", "vp", 0, "sq", "sp", a)
+        evict("ey%d" % c, ["my%d" % c], lambda T, a=a: T.yb[:, a:a + CH], "my%d" % c, None, ("ey%d" % c, 0))
 
     fin = ["qs%d_%d" % (c, HOPS) for c in range(NCH)]
     for c in range(NCH):
-        q = "Y" if c < NCH - 1 else "YS"
-        dma("o_c%d" % c, q, [fin[c]], lambda T, c=c: T.oc[:, 4 * CH * c:4 * CH * (c + 1)], lambda T, c=c: u8(T.sq[:, CH * c:CH * (c + 1)]),
-            128, 512 * CH, grp=("out", 0), fixed=False)
-        dma("o_y%d" % c, q, ["ey%d" % c], lambda T, c=c: T.y[:, CH * c:CH * (c + 1)], lambda T, c=c: T.yb[:, CH * c:CH * (c + 1)],
-            128, 512 * CH, grp=("out", 0), fixed=False)
-    dma("o_pl", "Y", ["pl%d_%d" % (c, HOPS - 1) for c in range(NCH)], lambda T: T.pl[:], lambda T: T.plb[0:128:16, :],
-        16, 12288, grp=("out", 0), fixed=False)
+        dma("o_c%d" % c, "YS", [fin[c]], lambda T, c=c: T.oc[:, 4 * CH * c:4 * CH * (c + 1)], lambda T, c=c: u8(T.sq[:, CH * c:CH * (c + 1)]),
+            128, 512 * CH, grp=("out", 0))
+        dma("o_y%d" % c, "YS", ["ey%d" % c], lambda T, c=c: T.y[:, CH * c:CH * (c + 1)], lambda T, c=c: T.yb[:, CH * c:CH * (c + 1)],
+            128, 512 * CH, grp=("out", 0))
+    dma("o_pl", "YS", ["pl%d_%d" % (c, HOPS - 1) for c in range(NCH)], lambda T: T.pl[:], lambda T: T.plb[0:128:16, :],
+        16, 12288, grp=("out", 0))
     for k in range(4):
         dma("o_s%d" % k, "YS", fin, lambda T, k=k: T.osc[4 * k:4 * k + 4, :], lambda T, k=k: T.sp[32 * k:32 * k + 4, :],
-            16, 1536, grp=("out", 0), fixed=False)
+            16, 1536, grp=("out", 0))
     return ops
-
-
-def link(ops):
-    by = {o["name"]: o for o in ops}
-    members, prev = {}, {}
-    for o in ops:
-        members.setdefault(o["grp"], []).append(o["name"])
-    for o in ops:
-        o["need"] = sorted(set(m for d in o["deps"] for m in members[by[d]["grp"]]))
-        o["before"] = [prev[q] for q in o["q"] if q in prev and (o["fixed"] or o["cost"][0] == "dma")]
-        if o["fixed"]:
-            prev[o["q"]] = o["name"]
-    return by, members
 
 
 def arrange(plan):
     ops = build_ops()
-    by, members = link(ops)
+    by = {o["name"]: o for o in ops}
     order, place = [], {}
     for word in plan.split():
         o = by[word[1:]]
         o["on"] = word[0]
         place[o["name"]] = len(order)
         order.append(o)
+    reader = {o["reads"]: o for o in ops if o["reads"]}
+    members = {}
+    for o in ops:
+        members.setdefault(o["grp"], []).append(o["name"])
+    bank, holder, uses, flags, acc = {}, [None] * BANKS, [0] * BANKS, {}, {}
+    for o in order:
+        key = o["acc"]
+        if key is None:
+            continue
+        acc.setdefault(key, []).append(o["name"])
+        if key not in bank:
+            freed = [-1 if h is None else max(place[m] for m in members[reader[h]["grp"]]) for h in holder]
+            b = freed.index(min(freed))
+            if holder[b] is not None:
+                o["deps"].append(reader[holder[b]]["name"])
+            bank[key], holder[b] = (b, uses[b]), key
+            uses[b] += 1
+    for o in ops:
+        if o["acc"]:
+            o["grp"] = ("bk%d" % bank[o["acc"]][0], bank[o["acc"]][1])
+        elif o["name"][:2] in ("ev", "er") and FINE:
+            o["grp"] = ("rd%d" % bank[o["reads"]][0], bank[o["reads"]][1])
+    members = {}
+    for o in ops:
+        members.setdefault(o["grp"], []).append(o["name"])
     known = {q: set() for q in "VSTYG"}
     seen, waited = {}, set()
     for o in order:
@@ -368,7 +351,7 @@ def arrange(plan):
             seen[o["name"]] = set()
             continue
         k = known[o["on"]]
-        for d in sorted(o["need"], key=lambda d: -place[d]):
+        for d in sorted(set(m for d in o["deps"] for m in members[by[d]["grp"]]), key=lambda d: -place[d]):
             if d in k:
                 continue
             g = by[d]["grp"]
@@ -378,78 +361,70 @@ def arrange(plan):
                 k.add(m)
                 k |= seen[m]
         seen[o["name"]] = set(k)
-    acc, flags = {}, {}
     for o in order:
-        if o["acc"]:
-            acc.setdefault(o["acc"], []).append(o["name"])
         o["raise"] = o["grp"] in waited or o["cost"][0] in ("dma", "call", "arr")
     for names in acc.values():
         for i, nm in enumerate(names):
             flags[nm] = (i == 0, i == len(names) - 1)
-    return order, flags
+    return order, flags, {key: b for key, (b, u) in bank.items()}
 
 
-ORDER, FLAGS = arrange(PLAN)
-SEMAPHORES = sorted(set(o["grp"][0] for o in ORDER if o["raise"]) | {"hnx", "hka", "hkb", "huq", "hup"})
+ORDER, FLAGS, BANK = arrange(PLAN) if PLAN.strip() else ([], {}, {})
+SEMAPHORES = sorted(set(o["grp"][0] for o in ORDER if o["raise"]) | {"hnx", "hka", "hkb", "hkp", "huq", "hup"})
 
 
 def roles(T, topo, r):
     me, one, two = T.cores[r], T.cores[(r - 1) % N], T.cores[(r - 2) % N]
     own = [c for c in topo.cores_of(me) if c != me and topo.may_write(c, one)]
-    near = [c for c in own if topo.die(c) == topo.die(me)][0]
-    other = [c for c in own if topo.die(c) != topo.die(me)][0]
-    far = [c for c in range(WORLD) if topo.mates(c, one) and topo.may_write(c, one) and topo.may_write(me, c)
-           and topo.may_write(c, two) and topo.die(c) != topo.die(me)][0]
-    return me, [near, other, far], one, two
+    same = [c for c in own if topo.die(c) == topo.die(me)]
+    other = [c for c in own if topo.die(c) != topo.die(me)]
+    return me, [same[0], other[0], same[1], other[1]], one, two
 
 
-def halves(engines):
-    return engines[:len(engines) // 2], engines[len(engines) // 2:]
-
-
-def rank_sends(topo, me, hands, two):
-    off = topo.engines(me, hands[2])
+def rank_sends(topo, me, hands):
     every = topo.engines(me, hands[0])
-    ra, rb = halves([e for e in every if e not in off])
-    oa, ob = halves(off)
-    ea, eb = halves(every)
-    return {"hnx": [(0, ra), (1, rb), (2, oa), (2, ob)], "hka": [(0, ea), (1, eb)], "hkb": [(0, ra), (1, rb), (2, off)],
-            "huq": [(2, off)], "hup": [(2, off)], "a_u2": [(3, topo.engines(me, two))]}
+    q = len(every) // 4
+    return {"s_nx": [(j, every[q * j:q * (j + 1)]) for j in range(4)], "s_ka": [(0, every)], "s_kb": [(2, every[0::2]), (1, every[1::2])],
+            "s_kp": [(3, every)], "s_uq": [(0, every)], "s_up": [(3, every)]}
 
 
 def helper_program(g, core, T, topo, r, j):
     me, hands, one, two = roles(T, topo, r)
-    use = rank_sends(topo, me, hands, two)
-
-    def wait(key):
-        g.wait_ge(T.sem[key], sum(len(e) for who, e in use[key] if who == j))
-
+    use = rank_sends(topo, me, hands)
     eng = topo.engines(core, one)
     m, n = mask_of(eng), len(eng)
     a1, a2 = topo.addr(one, core), topo.addr(two, core)
-    d1, d2 = DstId(rid=a1[0], pnc=a1[1]), DstId(rid=a2[0], pnc=a2[1])
-    wait("hnx")
-    parts = [(0, j, eng)] if j < 2 else [(i, 2 + i, halves(eng)[i]) for i in range(2)]
-    g.remote_dma_fused([RemoteDMATransfer(dst_ids=[d1, d2], dma_engine_mask=mask_of(e), remote_sem=T.sem.a_nx, srcs=[T.hnx[i]],
-                                          dsts=[T.nd1[s], T.nd2[s]]) for i, s, e in parts], local_sem=T.sem.sent)
-    if j < 2:
-        cols = [QUART * j, HALF + QUART * j]
-        for i, key in enumerate(("hka", "hkb")):
-            wait(key)
-            g.remote_dma(u8(T.k1q[:, cols[i]:cols[i] + QUART]), u8(T.hq[:, QUART * i:QUART * (i + 1)]), T.sem.a_k1q, T.sem.sent, a1[1], a1[0], m)
-        g.remote_dma_fused([RemoteDMATransfer(
-            dst_ids=[d2], dma_engine_mask=mask_of(halves(eng)[i]), remote_sem=T.sem.a_k2q,
-            src=u8(T.hq[:, QUART * i:QUART * (i + 1)]), dst=u8(T.k2q[:, cols[i]:cols[i] + QUART])) for i in range(2)], local_sem=T.sem.sent)
-        calls = 4
+
+    def wait(key):
+        g.wait_ge(T.sem["h" + key], sum(len(e) for who, e in use["s_" + key] if who == j))
+
+    def send(dst, src, key, a):
+        g.remote_dma(dst, src, T.sem[key], T.sem.sent, a[1], a[0], m)
+
+    wait("nx")
+    g.remote_dma_fused([RemoteDMATransfer(dst_ids=[DstId(rid=a[0], pnc=a[1]) for a in (a1, a2)], dma_engine_mask=m, remote_sem=T.sem.a_nx,
+                                          srcs=[T.hnx[:]], dsts=[T.nd1[j], T.nd2[j]])], local_sem=T.sem.sent)
+    calls = 5
+    if j == 0:
+        wait("ka")
+        send(u8(T.k1q[:, 0:KA]), u8(T.hq[:, 0:KA]), "a_k1q", a1)
+        wait("uq")
+        send(u8(T.u1q[:]), u8(T.huq[:]), "a_u1", a1)
+        send(u8(T.k2q[:, 0:KA]), u8(T.hq[:, 0:KA]), "a_k2q", a2)
+        send(u8(T.u2q[:]), u8(T.huq[:]), "a_u2", a2)
+    elif j == 3:
+        wait("kp")
+        send(T.k1p[:], T.hp[:], "a_k1p", a1)
+        wait("up")
+        send(T.u1p[:], T.hup[:], "a_u1", a1)
+        send(T.k2p[:], T.hp[:], "a_k2p", a2)
+        send(T.u2p[:], T.hup[:], "a_u2", a2)
     else:
-        wait("hkb")
-        g.remote_dma(T.k1p[:], T.hp[:], T.sem.a_k1p, T.sem.sent, a1[1], a1[0], m)
-        wait("huq")
-        g.remote_dma(u8(T.u1q[:]), u8(T.huq[:]), T.sem.a_u1, T.sem.sent, a1[1], a1[0], m)
-        wait("hup")
-        g.remote_dma(T.u1p[:], T.hup[:], T.sem.a_u1, T.sem.sent, a1[1], a1[0], m)
-        g.remote_dma(T.k2p[:], T.hp[:], T.sem.a_k2p, T.sem.sent, a2[1], a2[0], m)
-        calls = 5
+        at = KA + KB * [who for who, e in use["s_kb"]].index(j)
+        wait("kb")
+        send(u8(T.k1q[:, at:at + KB]), u8(T.hq[:, 0:KB]), "a_k1q", a1)
+        send(u8(T.k2q[:, at:at + KB]), u8(T.hq[:, 0:KB]), "a_k2q", a2)
+        calls = 3
     g.wait_ge(T.sem.sent, calls * n)
 
 
@@ -462,18 +437,18 @@ def rank_program(g, core, T, topo):
                 helper_program(g, core, T, topo, r, hands.index(core))
         return
     me, hands, one, two = roles(T, topo, rank)
-    use = rank_sends(topo, me, hands, two)
-    C = {"acc": FLAGS, "addr": {j: topo.addr(c, me) for j, c in enumerate(hands + [two])}, "use": use}
+    use = rank_sends(topo, me, hands)
+    C = {"acc": FLAGS, "bank": BANK, "addr": [topo.addr(c, me) for c in hands], "use": use}
     n1 = [len(topo.engines(c, me)) for c in roles(T, topo, (rank + 1) % N)[1]]
     n2 = [len(topo.engines(c, me)) for c in roles(T, topo, (rank + 2) % N)[1]]
-    inc = {"a_nx": sum(n1) + sum(n2), "a_k1q": 2 * (n1[0] + n1[1]), "a_k1p": n1[2], "a_u1": 2 * n1[2],
-           "a_k2q": n2[0] + n2[1], "a_k2p": n2[2], "a_u2": 2 * len(topo.engines(T.cores[(rank + 2) % N], me)), "sig0": 1, "sig": 1}
-    for name, key in (("s_nx", "hnx"), ("s_ka", "hka"), ("s_kb", "hkb"), ("s_uq", "huq"), ("s_up", "hup"), ("s_uq2", "a_u2"), ("s_up2", "a_u2")):
-        inc[name] = sum(len(e) for who, e in use[key])
+    inc = {"a_nx": sum(n1) + sum(n2), "a_k1q": sum(n1[:3]), "a_k1p": n1[3], "a_u1": n1[0] + n1[3],
+           "a_k2q": sum(n2[:3]), "a_k2p": n2[3], "a_u2": n2[0] + n2[3]}
+    for name in use:
+        inc[name] = sum(len(e) for who, e in use[name])
     per = {}
     for o in ORDER:
         if o["raise"]:
-            per[o["grp"]] = per.get(o["grp"], 0) + (o["inc"] or inc[o["name"]])
+            per[o["grp"]] = per.get(o["grp"], 0) + (o["inc"] or inc.get(o["name"], 1))
     value, total = {}, {}
     for grp in sorted(per):
         total[grp[0]] = total.get(grp[0], 0) + per[grp]

from concourse.bass import DstId, RemoteDMATransfer
from concourse.mybir import dt, AluOpType, ActivationFunctionType

N, TOK, P, HOPS = 8, 384, 448, 3
CH = 128
NCH = TOK // CH
NL = CH // 16
NB = CH // 32
HALF = P // 2
KA = 140
KB = (P - KA) // 2
SEG = P // 16
NXW = 2 * P * 8 // 512
ZW, TW = CH + 32, 2 * CH + 32
PW = 32
LC = (3 * NL + 15) // 16
LW = 16 * LC
EW = 520
BANKS = 8
FINE = True
CODE, BF, F32, I32, U16, U8 = "float8_e4m3fn_x4", "bfloat16", "float32", "int32", "uint16", "uint8"

SCRATCH = {
    "xin": ("sbuf", [128, 4 * TOK], BF), "kin": ("sbuf", [128, 4 * P], BF),
    "uin": ("sbuf", [128, 512], BF), "vin": ("sbuf", [128, 512], BF),
    "wq": ("sbuf", [128, 512], CODE), "wp": ("sbuf", [128, 512], U8),
    "nxi": ("sbuf", [128, 2 * SEG], I32), "sti": ("sbuf", [128, TOK // 16], I32),
    "kq": ("sbuf", [128, P], CODE), "kp": ("sbuf", [128, P], U8),
    "uq": ("sbuf", [128, 128], CODE), "up": ("sbuf", [128, 128], U8),
    "u0q": ("sbuf", [128, 128], CODE), "u0p": ("sbuf", [128, 128], U8),
    "u1q": ("sbuf", [128, 128], CODE), "u1p": ("sbuf", [128, 128], U8),
    "u2q": ("sbuf", [128, 128], CODE), "u2p": ("sbuf", [128, 128], U8),
    "k1q": ("sbuf", [128, P], CODE), "k1p": ("sbuf", [128, P], U8),
    "k2q": ("sbuf", [128, P], CODE), "k2p": ("sbuf", [128, P], U8),
    "vq": ("sbuf", [128, 128], CODE), "vp": ("sbuf", [128, 128], U8),
    "nd0": ("dram", [4, 128, NXW], I32), "nd1": ("dram", [4, 128, NXW], I32), "nd2": ("dram", [4, 128, NXW], I32),
    "stg": ("sbuf", [128, 2 * P + 4], I32), "nxf": ("sbuf", [128, 2 * SEG], F32),
    "win0": ("sbuf", [128, P], BF), "win1": ("sbuf", [128, P], BF), "win2": ("sbuf", [128, 2 * P], F32),
    "dia": ("sbuf", [128, 128], BF), "cst": ("sbuf", [128, 96], F32), "cstt": ("sbuf", [128, 96], F32),
    "lay": ("sbuf", [128, 32 * LC], F32), "layt": ("sbuf", [128, 32 * LC], F32),
    "rep": ("sbuf", [128, 8], I32), "repo": ("sbuf", [128, 8], U16), "wrap": ("sbuf", [128, LC], U16),
    "et": ("sbuf", [128, 3 * EW], BF), "eq": ("sbuf", [128, 1536], CODE), "ep": ("sbuf", [128, 1536], U8),
    "o0": ("sbuf", [128, 5 * TOK // 16], U16), "off": ("sbuf", [128, LW * NCH], U16),
    "nt": ("sbuf", [128, 4 * TOK], BF), "vt": ("sbuf", [128, 4 * TOK], BF), "rt": ("sbuf", [128, 4 * TOK], BF),
    "nq": ("sbuf", [128, TOK], CODE), "npl": ("sbuf", [128, TOK], U8),
    "bq": ("sbuf", [128, TOK], CODE), "bp": ("sbuf", [128, TOK], U8),
    "sq": ("sbuf", [128, TOK], CODE), "sp": ("sbuf", [128, TOK], U8),
    "pq": ("sbuf", [128, 2 * TOK], CODE), "ppl": ("sbuf", [128, 2 * TOK], U8),
    "sel": ("sbuf", [128, TOK], BF), "zz": ("sbuf", [128, ZW * NCH], BF), "tt": ("sbuf", [128, TW * NCH], BF),
    "pw": ("sbuf", [128, PW * NCH], F32), "bd": ("sbuf", [128, TOK], F32), "plb": ("sbuf", [128, TOK], F32),
    "yb": ("sbuf", [128, TOK], F32),
    "hq": ("sbuf", [128, max(KA, KB)], CODE), "hp": ("sbuf", [128, P], U8),
    "huq": ("sbuf", [128, 128], CODE), "hup": ("sbuf", [128, 128], U8), "hnx": ("dram", [128, NXW], I32),
    "ps": ("psum", [128, 512 * BANKS], F32),
}

ALU, ACT = AluOpType, ActivationFunctionType

PLAN = """
Sl_nx Yl_k0 Gi_d Vz_e Sl_st Yl_k1 Yl_x0 Yl_u Yl_x1 Gi_c0 Ve0 Gi_c1 Gi_c2 Gz_s0 Vq_e03 Vc_t Vq_e00 Vq_e02 Vz_s1 Gs_nx Yga0 Se1 Se2 Sga1 Vc_o1 Vq_e01 Vc_o2 Vc_o3 Vq_k0 Vc_o4 Gi_rep Gs_ka Vc_o0 Vq_e20 Vq_k1 Gs_kb Vg20_0 Vqs0_0 Vg22_0 Vg30_0 Sg00_0 Sg32_0 Sg02_0 Sg12_0 Gs_kp Gsgkp Gi_l0 Gi_l1 Yl_x2 Tms20_0 Tms10_0 Tms30_0 Yl_wc Gi_l2 Yl_ws Sg10_0 Sg01_0 Sg21_0 Sg11_0 Sg31_0 Vc_rep Vq_u Vqs1_0 Vqn0 Vqn2 Vp_uq Vq_e21 Gs_uq Tmn030_0 Tms01_0 Vq_e10 Vq_e13 Tmn010_0 Tmn000_0 Tms00_0 Tms11_0 Tms31_0 Tmn020_0 Tmn002_0 Sp_up Vq_e23 Vqn1 Vq_e12 Sev00_0 Vev30_0 Sev10_0 Sev20_0 Vq_e11 Vq_e22 Gs_up Tmn011_0 Tmn001_0 Gz_zz Sev11_0 Tmn021_0 Tmn031_0 Tmn022_0 Tms21_0 Sev01_0 Aa_nx Sev31_0 Sev21_0 Vqv0_0 Vqs2_0 Vc_w0 Tmu0_0 Tms32_0 Tms22_0 Tms02_0 Tmn012_0 Tmn032_0 Tms12_0 Gi_l3 Vsl0_0 Sev02_0 Sev22_0 Gi_l4 Vqv1_0 Aa_k1q Ygb0 Aa_k1p Ygb1 Gi_l5 Yl_n2 Sev12_0 Yl_v Vzz0_0 Gz_w2 Tmu1_0 Sev32_0 Vc_u Tml00_0 Tml10_0 Vsl1_0 Vtb0_0 Vqv2_0 Ser00_0 Ser10_0 Tmu2_0 Tml20_0 Vzz1_0 Vc_l Vta0_0 Ser20_0 Tml01_0 Tml30_0 Tml11_0 Aa_k2q Aa_u1 Vta1_0 Vsl2_0 Vtb1_0 Vpw0_0 Vzz2_0 Ser30_0 Tml12_0 Tml22_0 Tml32_0 Tml31_0 Vpw1_0 Vof0_0 Ser01_0 Ser11_0 Ser31_0 Aa_u2 Ser22_0 Vqs0_1 Vta2_0 Vof1_0 Spp0_1 Vpq0_1 Tms30_1 Tml02_0 Tml21_0 Tms10_1 Tms20_1 Tms00_1 Aa_k2p Ser21_0 Spp1_1 Vtb2_0 Vpq1_1 Tmn200_1 Tmn100_1 Tmn120_1 Tmn230_1 Tmn220_1 Tmn210_1 Tmn110_1 Vpw2_0 Sev00_1 Ser02_0 Vqs1_1 Sev20_1 Tmn130_1 Tmn131_1 Tmn201_1 Tms11_1 Tmn221_1 Tmn121_1 Tms21_1 Tms01_1 Tms31_1 Vof2_0 Vc_w1 Sev10_1 Sev30_1 Tmn111_1 Tmn101_1 Vqv0_1 Vpq2_1 Tmu0_1 Tmn211_1 Tmn231_1 Spp2_1 Ser32_0 Ser12_0 Sev21_1 Vsl0_1 Vqs2_1 Vc_f1 Tml00_1 Vzz0_1 Sev01_1 Sev31_1 Sev11_1 Tml20_1 Tmn232_1 Tml10_1 Tmn212_1 Tms32_1 Tmn132_1 Tmn222_1 Tmn122_1 Tms12_1 Tmn112_1 Vqv1_1 Vta0_1 Vtb0_1 Tmu1_1 Vq_v Tms02_1 Tms22_1 Tmn102_1 Tmn202_1 Vpw0_1 Ser20_1 Ser10_1 Sev32_1 Ser00_1 Sev12_1 Vsl1_1 Vof0_1 Vc_f0 Sev22_1 Tml30_1 Vzz1_1 Sev02_1 Yw20 Yw21 Tml21_1 Tml11_1 Tml31_1 Ser30_1 Vqv2_1 Vtb1_1 Vta1_1 Vqs0_2 Vpq0_2 Tml02_1 Tmu2_1 Tml01_1 Tml12_1 Tml22_1 Ser11_1 Ser31_1 Spp0_2 Ser01_1 Ser21_1 Vpw1_1 Vsl2_1 Vof1_1 Vqs1_2 Ser02_1 Ser22_1 Tms00_2 Tms10_2 Tml32_1 Ser32_1 Ser12_1 Vzz2_1 Tmn100_2 Tmn200_2 Tms20_2 Tmn230_2 Tmn110_2 Tmn220_2 Tms21_2 Tms30_2 Spp1_2 Tmn210_2 Tms31_2 Tms01_2 Tmn130_2 Tmn120_2 Vpq1_2 Vtb2_1 Vta2_1 Sev10_2 Sev00_2 Sev30_2 Sev20_2 Tmn201_2 Tmn101_2 Tmn221_2 Tmn121_2 Vqs2_2 Vpw2_1 Sev01_2 Vof2_1 Sev21_2 Vqv0_2 Spp2_2 Vpq2_2 Tmn131_2 Tmn111_2 Tmn211_2 Tms02_2 Tmn231_2 Tms22_2 Sev31_2 Tml10_2 Tmu0_2 Vsl0_2 Tml30_2 Tms11_2 Tml00_2 Ser30_2 Vev11_2 Vbd0_2 Ser00_2 Vqv1_2 Tmn222_2 Tmn102_2 Tml20_2 Tmn212_2 Tmn122_2 Ser20_2 Ser10_2 Vpl0_2 Sev22_2 Tmn232_2 Tmn132_2 Tms32_2 Tms12_2 Tmn112_2 Tmn202_2 Vqs0_3 Sev32_2 Tml01_2 Tml31_2 Vev02_2 Sev12_2 Yo_c0 Tml21_2 Tml11_2 Tmy0 Ver31_2 Ser01_2 Vqv2_2 Tmu1_2 Ser21_2 Ver11_2 Sey0 Vsl1_2 Tml22_2 Tml32_2 Vqs1_3 Yo_y0 Tml02_2 Tml12_2 Ser22_2 Vbd1_2 Tmu2_2 Ser32_2 Yo_c1 Tmy1 Ver02_2 Ser12_2 Vsl2_2 Sey1 Vqs2_3 Vbd2_2 Yo_y1 Tmy2 Yo_c2 Yo_s0 Vpl1_2 Sey2 Yo_s1 Vpl2_2 So_y2 Yo_s2 Yo_s3 So_pl
"""

GATE = {"l_x2": ["sgkp"]}


def mask_of(engines):
    m = 0
    for e in engines:
        m |= 1 << e
    return m


def u8(v):
    return v.bitcast(dt.uint8)


def u32(v):
    return v.bitcast(dt.uint32)


def build_ops():
    ops = []

    def op(name, q, c, deps, fn, grp=None, inc=1, acc=None, reads=None):
        ops.append({"name": name, "q": q, "cost": c, "deps": list(deps) + GATE.get(name, []), "fn": fn, "grp": grp or (name, 0),
                    "inc": inc, "acc": acc, "reads": reads})

    def dma(name, q, deps, out, src, rows, size, grp=None):
        op(name, q, ("dma", (rows, size)), deps, lambda q_, e, T, C: e.dma_start(out(T), src(T)), grp=grp, inc=16)

    def bank(T, C, key):
        return T.ps[:, 512 * C["bank"][key]:512 * C["bank"][key] + CH]

    def scaled(q_, e, out, src, by):
        if q_ == "V":
            return e.tensor_copy(out, src) if by is None else e.tensor_scalar(out, src, by, None, ALU.mult)
        return e.activation(out, src, ACT.Copy) if by is None else e.activation(out, src, ACT.Copy, scale=by)

    def evict(name, deps, out, key, by, grp):
        op(name, "SV", ("el", CH), deps, lambda q_, e, T, C: scaled(q_, e, out(T), bank(T, C, key), by), grp=grp, reads=key)

    def moved(out, src):
        return lambda q_, e, T, C: scaled(q_, e, out(T), src(T), None)

    def quant(name, deps, cq, cp, a, n, tile, grp=None, src=None):
        b = 4 * a if src is None else src
        op(name, "V", ("q", n), deps,
           lambda q_, e, T, C: e.quantize_mx(T[cq][:, a:a + n], T[cp][:, a:a + n], T[tile][:, b:b + 4 * n]), grp=grp)

    def mm(name, deps, key, wq, wp, wa, xq, xp, xa):
        def fn(q_, e, T, C):
            first, last = C["acc"][name]
            return e.matmul_mx(bank(T, C, key), T[wq][:, wa:wa + 128], T[wp][:, wa:wa + 128],
                               T[xq][:, xa:xa + CH], T[xp][:, xa:xa + CH], first, last)
        op(name, "T", ("mm", CH), deps, fn, grp=(key, 0), acc=key)

    def stage(name, deps, src):
        for b in range(2):
            dma("%s%d" % (name, b), "YS", deps, lambda T, b=b: T.stg[b:128:16, 1 - b:1 - b + 2 * P], src, 16, 28672, grp=(name, 0))

    cut = (0, KA, P)
    dma("l_nx", "YS", [], lambda T: T.nd0[:], lambda T: T.nx[:], 16, 28672)
    dma("l_st", "YS", [], lambda T: T.sti[:], lambda T: T.st[:], 128, 12288)
    for h in range(2):
        dma("l_k%d" % h, "Y", [], lambda T, h=h: T.kin[:, 4 * cut[h]:4 * cut[h + 1]], lambda T, h=h: T.k[:, 4 * cut[h]:4 * cut[h + 1]],
            128, 1024 * (cut[h + 1] - cut[h]))
    for c in range(NCH):
        dma("l_x%d" % c, "Y", [], lambda T, c=c: T.xin[:, 4 * CH * c:4 * CH * (c + 1)], lambda T, c=c: T.x[:, 4 * CH * c:4 * CH * (c + 1)],
            128, 1024 * CH)
    dma("l_u", "Y", [], lambda T: T.uin[:], lambda T: T.u[:], 128, 131072)
    stage("ga", ["z_s0"], lambda T: T.nx[:])
    dma("l_wc", "Y", [], lambda T: u8(T.wq[:]), lambda T: T.wc[:], 128, 262144)
    dma("l_ws", "Y", [], lambda T: T.wp[:], lambda T: T.ws[:], 128, 65536)
    stage("gb", ["a_nx", "c_w0"], lambda T: T.nd1[:])
    dma("l_n2", "Y", ["a_nx"], lambda T: T.nxi[:], lambda T: T.nd2[:], 128, 28672)
    dma("l_v", "Y", [], lambda T: T.vin[:], lambda T: T.v[:], 128, 131072)
    for b in range(2):
        dma("w2%d" % b, "Y", ["c_f0", "z_w2"], lambda T, b=b: T.win2[0:128:16, P * b:P * (b + 1)],
            lambda T, b=b: T.nxf[:, SEG * b:SEG * (b + 1)], 128, 14336, grp=("w2", 0))

    def iota(name, out, pat, base, cm, n, small=True, grp=None):
        if small:
            fn = lambda q_, e, T, C: e.iota(out(T), pat, base, cm, allow_small_or_imprecise_dtypes=True)
        else:
            fn = lambda q_, e, T, C: e.iota(out(T), pat, base, cm)
        op(name, "G", ("iota", n), [], fn, grp=grp)

    def zero(name, out, n, narrow=False, small=True, grp=None):
        def fn(q_, e, T, C):
            if q_ == "V":
                return e.memset(out(T), 0.0 if small else 0)
            if small:
                return e.iota(out(T), [[0, n]], 0, 0, allow_small_or_imprecise_dtypes=True)
            return e.iota(out(T), [[0, n]], 0, 0)
        op(name, "GV", ("fill", (n, narrow)), [], fn, grp=grp)

    def remote(name, deps, src, dst, size):
        def fn(q_, e, T, C):
            return e.remote_dma_fused([RemoteDMATransfer(
                dst_ids=[DstId(rid=C["addr"][who][0], pnc=C["addr"][who][1])], dma_engine_mask=mask_of(engines),
                remote_sem=T.sem["h" + name[2:]], src=src(T, i), dst=dst(T)) for i, (who, engines) in enumerate(C["use"][name])],
                local_sem=T.sem.sent)
        op(name, "G", ("call", size), deps, fn, grp=("sent", 0), inc=None)

    iota("i_d", lambda T: T.dia[:], [[1, 128]], 0, -1, 128)
    for i in range(2):
        zero("z_s%d" % i, lambda T, i=i: T.stg[:, P * i + 1:P * (i + 1) + 1:2], HALF, small=False, grp=("z_s", 0))
    remote("s_nx", ["l_nx"], lambda T, i: T.nd0[i], lambda T: T.hnx[:], 28672)
    remote("s_ka", ["q_k0"], lambda T, i: u8(T.kq[:, 0:KA]), lambda T: u8(T.hq[:, 0:KA]), 512 * KA)
    remote("s_kb", ["q_k1"], lambda T, i: u8(T.kq[:, KA + KB * i:KA + KB * (i + 1)]), lambda T: u8(T.hq[:, 0:KB]), 1024 * KB)
    remote("s_kp", ["q_k0", "q_k1"], lambda T, i: T.kp[:], lambda T: T.hp[:], 128 * P)
    remote("s_uq", ["p_uq"], lambda T, i: u8(T.u0q[:]), lambda T: u8(T.huq[:]), 65536)
    remote("s_up", ["p_up"], lambda T, i: T.u0p[:], lambda T: T.hup[:], 16384)
    for name in sorted(set(v[0] for v in GATE.values())):
        op(name, "G", ("sig", "s_" + name[2:]), [], lambda q_, e, T, C, name=name: e.sem_inc(T.sem[name], 1), inc=None)
    iota("i_rep", lambda T: T.rep[:], [[16, 8]], 0, 0, 8, small=False)
    iota("i_c0", lambda T: T.cst[:, 0:32], [[0, 16], [1, 2]], 0, 0, 32, grp=("i_c", 0))
    iota("i_c1", lambda T: T.cst[:, 32:64], [[-1, 2], [0, 16]], 1, 0, 32, grp=("i_c", 0))
    iota("i_c2", lambda T: T.cst[:, 64:96], [[1, 2], [0, 16]], 0, 0, 32, grp=("i_c", 0))
    count = 0
    for odd in range(2):
        for e0 in range(3 * NL):
            s, c = e0 // NL, e0 % NL
            if e0 % 16 and c:
                continue
            n = min(16 - e0 % 16, NL - c)
            times = (16 - e0 % 16) // n if e0 + n == 3 * NL else 1
            at = 32 * (e0 // 16) + 16 * odd + e0 % 16
            iota("i_l%d" % count, lambda T, at=at, w=n * times: T.lay[:, at:at + w],
                 [[0, times], [2, n // 2], [-2 * NB if odd else 2 * NB + 2, 2]], c + (s if s < 2 else odd) + 2 * NB * odd, 0, n * times,
                 grp=("i_l", 0))
            count += 1
    zero("z_zz", lambda T: T.zz[:], ZW * NCH, narrow=True)
    zero("z_w2", lambda T: T.win2[:], 2 * P)

    for name, after in (("a_nx", []), ("a_k1q", ["s_ka", "s_kb"]), ("a_k1p", ["s_kp"]), ("a_u1", ["s_ka", "s_kp", "s_uq", "s_up"]),
                        ("a_k2q", ["s_ka", "s_kb", "s_uq"]), ("a_k2p", ["s_kp", "s_up"]), ("a_u2", ["s_ka", "s_kp", "s_uq", "s_up"])):
        op(name, "A", ("arr", ["s_nx"] + after), [], None, inc=None)

    op("z_e", "V", ("el", EW // 2), [], lambda q_, e, T, C: e.memset(T.et[:, 0:EW], 0.0))
    op("e0", "V", ("el", 64), ["i_d", "z_e"], lambda q_, e, T, C: e.tensor_scalar(T.et[:, 3:515:4], T.dia[:], 0.0, None, ALU.is_equal))
    op("c_t", "V", ("el", 96), ["i_c0"], lambda q_, e, T, C: e.transpose(T.cstt[:], T.cst[:]))
    op("c_u", "V", ("el", 32 * LC), ["i_l0"], lambda q_, e, T, C: e.transpose(T.layt[:], T.lay[:]))
    op("c_l", "V", ("el", LC), ["c_u"], lambda q_, e, T, C: e.tensor_copy(T.wrap[:], T.layt[:, 0:32 * LC:32]))
    op("c_rep", "V", ("el", 8), ["i_rep"], lambda q_, e, T, C: e.tensor_copy(T.repo[:], T.rep[:]))
    for s in range(3):
        if s:
            op("e%d" % s, "SV", ("el2", EW), ["e0", "c_t"], lambda q_, e, T, C, s=s: scaled(
                q_, e, T.et[:, EW * s:EW * (s + 1)], T.et[:, 0:EW], T.cstt[:, 32 * s:32 * s + 1]))
        for b in range(4):
            quant("q_e%d%d" % (s, b), ["e%d" % s], "eq", "ep", 512 * s + 128 * b, 128, "et", src=EW * s + 3 - b, grp=("q_e%d" % s, 0))

    for b in range(2):
        quant("q_k%d" % b, ["l_k%d" % b], "kq", "kp", cut[b], cut[b + 1] - cut[b], "kin")
        op("c_w%d" % b, "V", ("el", P), ["ga0" if b == 0 else "gb0"], lambda q_, e, T, C, b=b: e.tensor_scalar(
            T["win%d" % b][:], T.stg[:, 1:2 * P + 1:2], float(-HALF), None, ALU.add))
    W = TOK // 16
    for t in range(4):
        op("c_o%d" % t, "V", ("el", W), ["l_st"], lambda q_, e, T, C, t=t: e.tensor_scalar(
            T.o0[:, W * t:W * (t + 1)], T.sti[:], 4.0, float(t), ALU.mult, ALU.add))
    op("c_o4", "V", ("el", W), ["l_st"], lambda q_, e, T, C: e.tensor_copy(T.o0[:, 4 * W:5 * W], T.sti[:]))
    quant("q_u", ["l_u"], "uq", "up", 0, 128, "uin")
    op("p_uq", "V", ("g", 128), ["q_u", "c_rep"],
       lambda q_, e, T, C: e.tensor_copy(u32(T.u0q[:]), u32(T.uq[:]).indirect(T.repo[:])))
    op("p_up", "SV", ("g", 128), ["q_u", "c_rep"], moved(lambda T: T.u0p[:], lambda T: T.up[:].indirect(T.repo[:])))
    quant("q_v", ["l_v"], "vq", "vp", 0, 128, "vin")
    op("c_f0", "V", ("el", SEG), ["l_n2"],
       lambda q_, e, T, C: e.tensor_copy(T.nxf[:, 0:SEG], T.nxi[:, 0:2 * SEG:2]), grp=("c_f", 0))
    op("c_f1", "V", ("el", 2 * SEG), ["l_n2"],
       lambda q_, e, T, C: e.tensor_tensor(T.nxf[:, SEG:2 * SEG], T.nxi[:, 1:2 * SEG:2], T.nxi[:, 0:2 * SEG:2], ALU.subtract), grp=("c_f", 0))

    for c in range(NCH):
        a = CH * c
        quant("qs%d_0" % c, ["l_x%d" % c], "sq", "sp", a, CH, "xin", grp=("qs%d" % c, 0))
        for t in range(HOPS):
            n = "%d_%d" % (c, t)
            if t == 0:
                for b in range(4):
                    op("g%d%s" % (b, n), "SV", ("g", CH), ["l_k0", "l_k1", "c_o%d" % b], moved(
                        lambda T, b=b, a=a: T.nt[:, 4 * a + b:4 * (a + CH):4],
                        lambda T, b=b, c=c: T.kin[:].indirect(T.o0[:, W * b + NL * c:W * b + NL * (c + 1)])), grp=("g%d" % c, 0))
                quant("qn%d" % c, ["g0" + n], "nq", "npl", a, CH, "nt")
                nodes = [(0, "nq", "npl", a, ["qn%d" % c])]
                nat = lambda T, c=c: T.o0[:, 4 * W + NL * c:4 * W + NL * (c + 1)]
                natdep = "c_o4"
            else:
                natdep = "of%d_%d" % (c, t - 1)
                lst = lambda T, c=c: T.off[:, LW * c:LW * c + 2 * NL]
                op("pq" + n, "V", ("g", 2 * CH), [natdep, "a_k%dq" % t], lambda q_, e, T, C, lst=lst, a=a, t=t: e.tensor_copy(
                    u32(T.pq[:, 2 * a:2 * (a + CH)]), u32(T["k%dq" % t][:]).indirect(lst(T))), grp=("pk%d" % c, t))
                op("pp" + n, "SV", ("g", 2 * CH), [natdep, "a_k%dp" % t], moved(
                    lambda T, a=a: T.ppl[:, 2 * a:2 * (a + CH)],
                    lambda T, lst=lst, t=t: T["k%dp" % t][:].indirect(lst(T))), grp=("pk%d" % c, t))
                nodes = [(1 + s, "pq", "ppl", 2 * a + CH * s, ["pq" + n]) for s in range(2)]
                nat = lambda T, c=c: T.off[:, LW * c + 2 * NL:LW * c + 3 * NL]
            for b in range(4):
                key = "bl%d%s" % (b, n)
                mm("ms%d%s" % (b, n), ["qs" + n, "q_e00"], key, "eq", "ep", 128 * b, "sq", "sp", a)
                for s, xq, xp, xa, deps in nodes:
                    mm("mn%d%d%s" % (s, b, n), deps + ["q_e%d0" % s], key, "eq", "ep", 512 * s + 128 * b, xq, xp, xa)
                evict("ev%d%s" % (b, n), ["ms%d%s" % (b, n)], lambda T, b=b, a=a: T.vt[:, 4 * a + b:4 * (a + CH):4], key, 0.5,
                      None if FINE else ("ev%d" % c, t))
            quant("qv" + n, ["ev%d%s" % (b, n) for b in range(4)], "bq", "bp", a, CH, "vt", grp=("qv%d" % c, t))
            udeps = ["p_uq", "p_up"] if t == 0 else ["a_u%d" % t]
            mm("mu" + n, ["qv" + n] + udeps, "mu" + n, "u%dq" % t, "u%dp" % t, 0, "bq", "bp", a)
            sel = lambda T, a=a: T.sel[:, a:a + CH]
            if t < HOPS - 1:
                op("sl" + n, "V", ("el", CH), ["mu" + n, "c_t"], lambda q_, e, T, C, n=n, sel=sel: e.tensor_scalar(
                    sel(T), bank(T, C, "mu" + n), 0.0, T.cstt[:, 0:1], ALU.is_gt, ALU.is_equal), grp=("sl%d" % c, t), reads="mu" + n)
                z, y = ZW * c, TW * c
                op("zz" + n, "V", ("g", CH), ["sl" + n, "c_w%d" % t, natdep, "z_zz"], lambda q_, e, T, C, z=z, t=t, nat=nat, sel=sel: e.tensor_tensor(
                    T.zz[:, z + 16:z + 16 + CH], T["win%d" % t][:].indirect(nat(T)), sel(T), ALU.mult), grp=("zz%d" % c, t))
                op("ta" + n, "V", ("el", CH // 2), ["zz" + n], lambda q_, e, T, C, z=z, y=y: e.transpose(
                    T.tt[:, y:y + CH], T.zz[:, z + 16:z + 16 + CH]), grp=("tt%d" % c, t))
                op("tb" + n, "V", ("el", ZW // 2), ["zz" + n], lambda q_, e, T, C, z=z, y=y: e.transpose(
                    T.tt[:, y + CH:y + TW], T.zz[:, z:z + ZW]), grp=("tt%d" % c, t))
                op("pw" + n, "V", ("el", TW // 8), ["ta" + n], lambda q_, e, T, C, c=c, y=y: e.tensor_tensor(
                    T.pw[:, PW * c:PW * c + TW // 16], T.tt[:, y:y + TW:16], T.tt[:, y + 1:y + TW:16], ALU.add), grp=("pw%d" % c, t))
                op("of" + n, "V", ("g", LW), ["pw" + n, "c_l"], lambda q_, e, T, C, c=c: e.tensor_scalar(
                    T.off[:, LW * c:LW * (c + 1)], T.pw[:, PW * c:PW * c + TW // 16].indirect(T.wrap[:]), float(HALF), None, ALU.add),
                   grp=("of%d" % c, t))
            else:
                op("sl" + n, "V", ("el", CH), ["mu" + n], lambda q_, e, T, C, n=n, sel=sel: e.tensor_scalar(
                    sel(T), bank(T, C, "mu" + n), 0.0, None, ALU.is_gt), grp=("sl%d" % c, t), reads="mu" + n)
                op("bd" + n, "V", ("g", CH), ["sl" + n, "w20", natdep], lambda q_, e, T, C, a=a, nat=nat, sel=sel: e.tensor_tensor(
                    T.bd[:, a:a + CH], T.win2[:, P:2 * P].indirect(nat(T)), sel(T), ALU.mult), grp=("zz%d" % c, t))
                op("pl" + n, "V", ("g", CH), ["bd" + n], lambda q_, e, T, C, a=a, nat=nat: e.tensor_tensor(
                    T.plb[:, a:a + CH], T.win2[:, 0:P].indirect(nat(T)), T.bd[:, a:a + CH], ALU.add), grp=("pw%d" % c, t))
            for b in range(4):
                key = "ml%d%s" % (b, n)
                mm(key, ["qv" + n, "l_wc", "l_ws"], key, "wq", "wp", 128 * b, "bq", "bp", a)
                evict("er%d%s" % (b, n), [key], lambda T, b=b, a=a: T.rt[:, 4 * a + b:4 * (a + CH):4], key, 0.03125,
                      None if FINE else ("er%d" % c, t))
            quant("qs%d_%d" % (c, t + 1), ["er%d%s" % (b, n) for b in range(4)], "sq", "sp", a, CH, "rt", grp=("qs%d" % c, t + 1))
        mm("my%d" % c, ["qs%d_%d" % (c, HOPS), "q_v"], "my%d" % c, "vq", "vp", 0, "sq", "sp", a)
        evict("ey%d" % c, ["my%d" % c], lambda T, a=a: T.yb[:, a:a + CH], "my%d" % c, None, ("ey%d" % c, 0))

    fin = ["qs%d_%d" % (c, HOPS) for c in range(NCH)]
    for c in range(NCH):
        dma("o_c%d" % c, "YS", [fin[c]], lambda T, c=c: T.oc[:, 4 * CH * c:4 * CH * (c + 1)], lambda T, c=c: u8(T.sq[:, CH * c:CH * (c + 1)]),
            128, 512 * CH, grp=("out", 0))
        dma("o_y%d" % c, "YS", ["ey%d" % c], lambda T, c=c: T.y[:, CH * c:CH * (c + 1)], lambda T, c=c: T.yb[:, CH * c:CH * (c + 1)],
            128, 512 * CH, grp=("out", 0))
    dma("o_pl", "YS", ["pl%d_%d" % (c, HOPS - 1) for c in range(NCH)], lambda T: T.pl[:], lambda T: T.plb[0:128:16, :],
        16, 12288, grp=("out", 0))
    for k in range(4):
        dma("o_s%d" % k, "YS", fin, lambda T, k=k: T.osc[4 * k:4 * k + 4, :], lambda T, k=k: T.sp[32 * k:32 * k + 4, :],
            16, 1536, grp=("out", 0))
    return ops


def arrange(plan):
    ops = build_ops()
    by = {o["name"]: o for o in ops}
    order, place = [], {}
    for word in plan.split():
        o = by[word[1:]]
        o["on"] = word[0]
        place[o["name"]] = len(order)
        order.append(o)
    reader = {o["reads"]: o for o in ops if o["reads"]}
    members = {}
    for o in ops:
        members.setdefault(o["grp"], []).append(o["name"])
    bank, holder, uses, flags, acc = {}, [None] * BANKS, [0] * BANKS, {}, {}
    for o in order:
        key = o["acc"]
        if key is None:
            continue
        acc.setdefault(key, []).append(o["name"])
        if key not in bank:
            freed = [-1 if h is None else max(place[m] for m in members[reader[h]["grp"]]) for h in holder]
            b = freed.index(min(freed))
            if holder[b] is not None:
                o["deps"].append(reader[holder[b]]["name"])
            bank[key], holder[b] = (b, uses[b]), key
            uses[b] += 1
    for o in ops:
        if o["acc"]:
            o["grp"] = ("bk%d" % bank[o["acc"]][0], bank[o["acc"]][1])
        elif o["name"][:2] in ("ev", "er") and FINE:
            o["grp"] = ("rd%d" % bank[o["reads"]][0], bank[o["reads"]][1])
    members = {}
    for o in ops:
        members.setdefault(o["grp"], []).append(o["name"])
    known = {q: set() for q in "VSTYG"}
    seen, waited = {}, set()
    for o in order:
        o["waits"] = []
        if o["on"] == "A":
            seen[o["name"]] = set()
            continue
        k = known[o["on"]]
        for d in sorted(set(m for d in o["deps"] for m in members[by[d]["grp"]]), key=lambda d: -place[d]):
            if d in k:
                continue
            g = by[d]["grp"]
            o["waits"].append(g)
            waited.add(g)
            for m in members[g]:
                k.add(m)
                k |= seen[m]
        seen[o["name"]] = set(k)
    for o in order:
        o["raise"] = o["grp"] in waited or o["cost"][0] in ("dma", "call", "arr")
    for names in acc.values():
        for i, nm in enumerate(names):
            flags[nm] = (i == 0, i == len(names) - 1)
    return order, flags, {key: b for key, (b, u) in bank.items()}


ORDER, FLAGS, BANK = arrange(PLAN) if PLAN.strip() else ([], {}, {})
SEMAPHORES = sorted(set(o["grp"][0] for o in ORDER if o["raise"]) | {"hnx", "hka", "hkb", "hkp", "huq", "hup"})


def roles(T, topo, r):
    me, one, two = T.cores[r], T.cores[(r - 1) % N], T.cores[(r - 2) % N]
    own = [c for c in topo.cores_of(me) if c != me and topo.may_write(c, one)]
    same = [c for c in own if topo.die(c) == topo.die(me)]
    other = [c for c in own if topo.die(c) != topo.die(me)]
    return me, [same[0], other[0], same[1], other[1]], one, two


def rank_sends(topo, me, hands):
    every = topo.engines(me, hands[0])
    q = len(every) // 4
    return {"s_nx": [(j, every[q * j:q * (j + 1)]) for j in range(4)], "s_ka": [(0, every)], "s_kb": [(2, every[0::2]), (1, every[1::2])],
            "s_kp": [(3, every)], "s_uq": [(0, every)], "s_up": [(3, every)]}


def helper_program(g, core, T, topo, r, j):
    me, hands, one, two = roles(T, topo, r)
    use = rank_sends(topo, me, hands)
    eng = topo.engines(core, one)
    m, n = mask_of(eng), len(eng)
    a1, a2 = topo.addr(one, core), topo.addr(two, core)

    def wait(key):
        g.wait_ge(T.sem["h" + key], sum(len(e) for who, e in use["s_" + key] if who == j))

    def send(dst, src, key, a):
        g.remote_dma(dst, src, T.sem[key], T.sem.sent, a[1], a[0], m)

    wait("nx")
    g.remote_dma_fused([RemoteDMATransfer(dst_ids=[DstId(rid=a[0], pnc=a[1]) for a in (a1, a2)], dma_engine_mask=m, remote_sem=T.sem.a_nx,
                                          srcs=[T.hnx[:]], dsts=[T.nd1[j], T.nd2[j]])], local_sem=T.sem.sent)
    calls = 5
    if j == 0:
        wait("ka")
        send(u8(T.k1q[:, 0:KA]), u8(T.hq[:, 0:KA]), "a_k1q", a1)
        wait("uq")
        send(u8(T.u1q[:]), u8(T.huq[:]), "a_u1", a1)
        send(u8(T.k2q[:, 0:KA]), u8(T.hq[:, 0:KA]), "a_k2q", a2)
        send(u8(T.u2q[:]), u8(T.huq[:]), "a_u2", a2)
    elif j == 3:
        wait("kp")
        send(T.k1p[:], T.hp[:], "a_k1p", a1)
        wait("up")
        send(T.u1p[:], T.hup[:], "a_u1", a1)
        send(T.k2p[:], T.hp[:], "a_k2p", a2)
        send(T.u2p[:], T.hup[:], "a_u2", a2)
    else:
        at = KA + KB * [who for who, e in use["s_kb"]].index(j)
        wait("kb")
        send(u8(T.k1q[:, at:at + KB]), u8(T.hq[:, 0:KB]), "a_k1q", a1)
        send(u8(T.k2q[:, at:at + KB]), u8(T.hq[:, 0:KB]), "a_k2q", a2)
        calls = 3
    g.wait_ge(T.sem.sent, calls * n)


def rank_program(g, core, T, topo):
    rank = T.rank_of(core)
    if rank is None:
        for r in range(N):
            hands = roles(T, topo, r)[1]
            if core in hands:
                helper_program(g, core, T, topo, r, hands.index(core))
        return
    me, hands, one, two = roles(T, topo, rank)
    use = rank_sends(topo, me, hands)
    C = {"acc": FLAGS, "bank": BANK, "addr": [topo.addr(c, me) for c in hands], "use": use}
    n1 = [len(topo.engines(c, me)) for c in roles(T, topo, (rank + 1) % N)[1]]
    n2 = [len(topo.engines(c, me)) for c in roles(T, topo, (rank + 2) % N)[1]]
    inc = {"a_nx": sum(n1) + sum(n2), "a_k1q": sum(n1[:3]), "a_k1p": n1[3], "a_u1": n1[0] + n1[3],
           "a_k2q": sum(n2[:3]), "a_k2p": n2[3], "a_u2": n2[0] + n2[3]}
    for name in use:
        inc[name] = sum(len(e) for who, e in use[name])
    per = {}
    for o in ORDER:
        if o["raise"]:
            per[o["grp"]] = per.get(o["grp"], 0) + (o["inc"] or inc.get(o["name"], 1))
    value, total = {}, {}
    for grp in sorted(per):
        total[grp[0]] = total.get(grp[0], 0) + per[grp]
        value[grp] = total[grp[0]]
    handle = {"V": g.vector, "S": g.scalar, "T": g.tensor, "Y": g.sync, "G": g}
    most = {}
    for o in ORDER:
        if o["on"] == "A":
            continue
        e = handle[o["on"]]
        for grp in o["waits"]:
            e.wait_ge(T.sem[grp[0]], value[grp])
            most[grp[0]] = max(most.get(grp[0], 0), value[grp])
        ins = o["fn"](o["on"], e, T, C)
        if o["raise"] and o["inc"]:
            ins.then_inc(T.sem[o["grp"][0]], o["inc"])
    for name in sorted(total):
        if most.get(name, 0) < total[name]:
            g.wait_ge(T.sem[name], total[name])
